import numpy as np, ml_dtypes
CORES = [16,18,20,22]
N = 4
BF = ml_dtypes.bfloat16
def gentries(a):
    return np.ascontiguousarray(a.reshape(8, 16, -1).transpose(0, 2, 1)).reshape(8, -1)
def gtable(e):
    e = np.asarray(e); return np.ascontiguousarray(e.reshape(8, -1, 16).transpose(0, 2, 1)).reshape(128, -1).astype(np.int32)
V, DV, M, DC, IT, CAP, B = 256, 3, 128, 6, 3, 224, 63
E = V * DV
def mixed(rng):
    c = np.full((N, N), E // N)
    for i in range(6 * N):
        p, p2 = rng.permutation(N)[:2]; q, q2 = rng.permutation(N)[:2]
        t = rng.integers(0, min(c[p, q2], c[p2, q], CAP - c[p, q], CAP - c[p2, q2]) + 1)
        c[p, q] += t; c[p2, q2] += t; c[p, q2] -= t; c[p2, q] -= t
    return c
def fullest(rng):
    odd = np.add.outer(rng.permutation(N), rng.permutation(N)) % 2
    return E // N + (CAP - E // N) * (1 - 2 * odd)
def fewest(rng):
    low = max(0, E - (N - 1) * CAP); each = (E - low) // (N - 1); more = E - low - each * (N - 1)
    w = np.concatenate([[low], each + (np.arange(N - 1) < more)]); k = rng.integers(1, N); p = np.arange(N)
    c = np.zeros((N, N), np.int64)
    for i in range(N): c[p, (p + k + i) % N] = w[i]
    return c
def graph(rng, ways, near=False, holes=False):
    sn = rng.integers(0, V, (N, 8, N * CAP)); pl = np.zeros((N, 8, E), np.int64); vl = np.zeros((N, 8, E), np.int64)
    def order(n, d):
        return np.add.outer(rng.permutation(n), n * np.arange(d)).reshape(-1) if near else rng.permutation(n * d)
    ve = [[order(V, DV) for r in range(N)] for g in range(8)]; ce = [[order(M, DC) for r in range(N)] for g in range(8)]
    c = ways(rng); va = np.add.accumulate(c, axis=1) - c; ca = np.add.accumulate(c, axis=0) - c
    for g in range(8):
        for p in range(N):
            for q in range(N):
                h = (g + p * q) % 8; n = int(c[p, q]); s = rng.permutation(CAP if holes else n)[:n]
                a = ve[g][p][va[p, q]:va[p, q] + n]; b = ce[h][q][ca[p, q]:ca[p, q] + n]
                vl[p, g, a] = q * CAP + s; pl[q, h, b] = p * CAP + s; sn[p, g, q * CAP + s] = a % V
    return {"sn": np.stack([gtable(e) for e in sn]), "pl": np.stack([gtable(e) for e in pl]), "vl": np.stack([gtable(e) for e in vl])}
def heard(rng):
    k = np.stack([rng.permutation(16) for g in range(8)]).reshape(1, 128, 1)
    mean = B * np.array([0, 0.1, 0.2, 0.7])[k // 4]; noise = B * np.array([0.1, 0.2, 0.4, 0.6])[k % 4]
    return (np.clip(np.rint(mean + noise * rng.standard_normal((N, 128, V))), -B, B) + 0.0).astype(BF)
def setup_inputs(rng):
    return {"x": heard(rng), **graph(rng, mixed)}
def setup_inputs_full(rng):
    return {"x": heard(rng), **graph(rng, fullest)}
def setup_inputs_holes(rng):
    return {"x": heard(rng), **graph(rng, fewest, holes=True)}
def setup_inputs_ties(rng):
    k = np.stack([rng.permutation(16) for g in range(8)]).reshape(1, 128, 1) % 4; z = (N, 128, V)
    sg = 2 * rng.integers(0, 2, z) - 1
    v = np.where(k == 0, sg, np.where(k == 1, rng.integers(-2, 3, z), np.where(k == 2, np.where(rng.random(z) < 0.1, -B, B), np.where(rng.random(z) < 0.0625, 0, B * sg))))
    return {"x": v.astype(BF), **graph(rng, mixed)}
def setup_inputs_twins(rng):
    return {"x": heard(rng), **graph(rng, mixed, near=True)}
def setup_inputs_spread(rng):
    hi = B >> rng.integers(0, 6, (N, 128, 1)); hi[:, ::16] = B
    v = rng.integers(-hi, hi + 1, (N, 128, V)) * (rng.random((N, 1, V)) > 0.0625)
    return {"x": v.astype(BF), **graph(rng, mixed, holes=True)}
def check_inputs(d):
    bad = []
    try:
        x = np.asarray(d["x"]).astype(np.float64)
        if not (np.isfinite(x).all() and (x == np.rint(x)).all() and (np.abs(x) <= B).all()): bad.append("x is whole and within B")
        sn, pl, vl = [np.stack([gentries(np.asarray(d[k][r])) for r in range(N)]).astype(np.int64) for k in ("sn", "pl", "vl")]
        if sn.min() < 0 or sn.max() >= V: bad.append("sn in range")
        if min(pl.min(), vl.min()) < 0 or max(pl.max(), vl.max()) >= N * CAP: return bad + ["pl and vl in range"]
        name = True; v = np.arange(E) % V
        uv = np.zeros((8, N, N * CAP), np.int64); uc = np.zeros((8, N, N * CAP), np.int64)
        for g in range(8):
            for r in range(N):
                uv[g, r] = np.bincount(vl[r, g], minlength=N * CAP); uc[g, r] = np.bincount(pl[r, g], minlength=N * CAP)
                name = name and bool((sn[r, g][vl[r, g]] == v).all())
        a = np.arange(N); h = (np.arange(8)[:, None, None] + np.multiply.outer(a, a)) % 8
        there = uc.reshape(8, N, N, CAP).transpose(0, 2, 1, 3)[h, a[:, None], a] > 0
        if max(uv.max(), uc.max()) > 1: bad.append("entries of pl and of vl differ")
        if not ((uv.reshape(8, N, N, CAP) > 0) == there).all(): bad.append("vl and pl name the same slots")
        if not name: bad.append("sn names the variable of each slot")
    except Exception:
        bad.append("shapes")
    return bad
def reference(x, sn, pl, vl):
    g = np.arange(8)[:, None, None]; r = np.arange(N)[:, None]
    ve = np.stack([gentries(vl[p]).astype(np.int64) for p in range(N)], axis=1) + (g * N + r) * N * CAP
    k = np.stack([gentries(pl[q]).astype(np.int64) for q in range(N)], axis=1); p = k // CAP
    ce = (((g - p * r) % 8 * N + p) * N + r) * CAP + k % CAP
    u = x.astype(np.float32).astype(np.int64).reshape(N, 8, 16, V).transpose(2, 1, 0, 3)
    back = np.zeros((16, 8 * N * N * CAP), np.int64); there = np.zeros((16, 8 * N * N * CAP), np.int64); tot = u
    for i in range(IT):
        there[:, ve] = np.clip(np.tile(tot, (1, 1, 1, DV)) - back[:, ve], -B, B)
        m = there[:, ce].reshape(16, 8, N, DC, M); size = np.abs(m); neg = (m < 0).astype(np.int64); new = np.zeros_like(m)
        for e in range(DC):
            o = [j for j in range(DC) if j != e]
            new[:, :, :, e] = np.min(size[:, :, :, o], axis=3) * (1 - 2 * (np.add.reduce(neg[:, :, :, o], axis=3) % 2))
        back[:, ce] = new.reshape(16, 8, N, E)
        tot = u + np.add.reduce(back[:, ve].reshape(16, 8, N, DV, V), axis=3)
    return {"y": np.ascontiguousarray(tot.transpose(2, 1, 0, 3)).reshape(N, 128, V).astype(np.float32)}

@@ -1,0 +1,349 @@
+import numpy as np
+from concourse.bass import DstId, RemoteDMATransfer
+from concourse.mybir import AluOpType as A, ActivationFunctionType as F
+
+N, V, M, CAP = 4, 256, 128, 224
+E = 768
+S4 = N * CAP
+H = E // 2
+SCRATCH = {
+    "snI": ("sbuf", [128, 56], "int32"), "plI": ("sbuf", [128, 48], "int32"), "vlI": ("sbuf", [128, 48], "int32"),
+    "xb": ("sbuf", [128, V], "bfloat16"),
+    "sn16": ("sbuf", [128, 56], "uint16"), "pl16": ("sbuf", [128, 48], "uint16"), "vl16": ("sbuf", [128, 48], "uint16"),
+    "ones": ("sbuf", [128, 256], "bfloat16"), "E2": ("sbuf", [128, 256], "bfloat16"), "E2f": ("sbuf", [128, 256], "float32"),
+    "BO": ("sbuf", [128, 128], "bfloat16"), "BO2": ("sbuf", [128, 128], "bfloat16"), "BOf": ("sbuf", [128, 128], "float32"),
+    "kkI": ("sbuf", [128, 48], "int32"), "kk16": ("sbuf", [128, 48], "uint16"),
+    "dg": ("sbuf", [128, 16], "int32"), "dg2": ("sbuf", [128, 16], "int32"),
+    "mask": ("sbuf", [128, E], "bfloat16"), "seg": ("sbuf", [128, E], "bfloat16"),
+    "XS": ("sbuf", [128, S4], "bfloat16"), "XW": ("sbuf", [128, S4], "bfloat16"), "xe": ("sbuf", [128, E], "bfloat16"),
+    "vt": ("sbuf", [128, 48], "float32"), "Qw": ("sbuf", [128, 48], "float32"), "QB": ("sbuf", [128, E], "float32"),
+    "QF": ("sbuf", [128, E], "float32"), "QS": ("sbuf", [128, S4], "float32"), "QW": ("sbuf", [128, S4], "float32"),
+    "QG": ("sbuf", [128, E], "float32"), "QC": ("sbuf", [128, E], "float32"), "qi": ("sbuf", [128, 48], "int32"),
+    "ee": ("sbuf", [128, 96], "int32"), "g1": ("sbuf", [128, 96], "float32"), "g2": ("sbuf", [128, 96], "float32"),
+    "g3": ("sbuf", [128, 96], "float32"), "g4": ("sbuf", [128, 96], "float32"), "LL": ("sbuf", [128, 96], "uint16"),
+    "k1": ("sbuf", [128, 48], "float32"), "k2": ("sbuf", [128, 48], "float32"), "k3": ("sbuf", [128, 48], "float32"),
+    "pp": ("sbuf", [128, 96], "float32"),
+    "W1": ("sbuf", [128, N * S4], "bfloat16"), "W2": ("sbuf", [128, N * S4], "bfloat16"),
+    "R3": ("sbuf", [128, S4], "bfloat16"), "VW": ("sbuf", [128, S4], "bfloat16"),
+    "yt": ("sbuf", [128, E], "bfloat16"), "yo": ("sbuf", [128, V], "float32"),
+}
+for _t in "123":
+    for _n, _w in (("t", E), ("r", E), ("c", H), ("s", E), ("aA", H), ("aB", H), ("L", 256), ("z", E), ("mg", E)):
+        SCRATCH[_n + _t] = ("sbuf", [128, _w], "bfloat16")
+    for _n in ("f1", "f2", "f3"):
+        SCRATCH[_n + "_" + _t] = ("sbuf", [128, M], "bfloat16")
+BANKS = ["b%d" % i for i in range(8)]
+for _b in BANKS:
+    SCRATCH[_b] = ("psum", [128, 512], "float32")
+SEMAPHORES = ["cv", "cs", "cp", "cg", "dsn", "dx", "dpl", "dvl", "dy0", "dy1", "lx", "lq", "l1", "l2", "l3"]
+SEMAPHORES += ["%s%d" % (k, p) for k in ("ax", "aq", "a1_", "a2_", "a3_") for p in range(N)]
+COMPUTE = {"v": "cv", "s": "cs", "p": "cp", "g": "cg"}
+
+
+def tracker(g, T):
+    eng = {"v": g.vector, "s": g.scalar, "p": g.tensor, "g": g, "y": g.sync}
+    acc, clk, done, cnt = {}, {q: {} for q in eng}, {}, {}
+
+    def wait(q, req):
+        for s in sorted(req):
+            if any(o != s and done.get((o, req[o]), {}).get(s, 0) >= req[s] for o in req):
+                continue
+            if clk[q].get(s, 0) < req[s]:
+                eng[q].wait_ge(T.sem[s], req[s])
+        for s in req:
+            for k, v in list(done.get((s, req[s]), {}).items()) + [(s, req[s])]:
+                clk[q][k] = max(clk[q].get(k, 0), v)
+
+    def needs(q, who, reads, writes):
+        req = {}
+        for lst, w in ((reads, False), (writes, True)):
+            for b, lo, hi in lst:
+                bank = b in BANKS
+                for (l2, h2, w2, q2, s, v) in acc.get(b, []):
+                    same = q2 == who
+                    if bank and not same:
+                        hit = True
+                    else:
+                        hit = (w or w2) and lo < h2 and l2 < hi
+                        if same and (not w2 or (bank and who == "p")):
+                            hit = False
+                    if hit:
+                        req[s] = max(req.get(s, 0), v)
+        return req
+
+    def note(who, reads, writes, s, v):
+        for lst, w in ((reads, False), (writes, True)):
+            for b, lo, hi in lst:
+                acc.setdefault(b, []).append((lo, hi, w, who, s, v))
+
+    def op(q, call, reads, writes, sem=None, inc=16):
+        who = q if sem is None else "dma"
+        wait(q, needs(q, who, reads, writes))
+        if sem is None:
+            sem, inc = COMPUTE[q], 1
+        cnt[sem] = cnt.get(sem, 0) + inc
+        r = call()
+        if r is not None:
+            r.then_inc(T.sem[sem], inc)
+        note(who, reads, writes, sem, cnt[sem])
+        c = dict(clk[q]); c[sem] = cnt[sem]
+        if who != "dma":
+            done[(sem, cnt[sem])] = c
+
+    def arrive(sem, n, region):
+        cnt[sem] = cnt.get(sem, 0) + n
+        note("rx", [], [region], sem, cnt[sem])
+
+    def finish():
+        wait("g", dict(cnt))
+    return op, arrive, finish
+
+
+def rank_program(g, core, T, topo):
+    me = T.rank_of(core)
+    if me is None:
+        return
+    op, arrive, finish = tracker(g, T)
+    vec, sca, ten = g.vector, g.scalar, g.tensor
+    others = sorted([r for r in range(N) if r != me], key=lambda r: (topo.die(T.cores[r]) != topo.die(core), (r - me) % N))
+
+    def ap(r):
+        return T[r[0]][:, r[1]:r[2]]
+
+    def full(n):
+        return (n, 0, SCRATCH[n][1][1])
+
+    def blk(name, k):
+        return (name, k * CAP, k * CAP + CAP)
+
+    def ind(r, l):
+        return ap(r).indirect(ap(l))
+
+    def vcopy(o, i): op("v", lambda: vec.tensor_copy(ap(o), ap(i)), [i], [o])
+    def vset(o, c): op("v", lambda: vec.memset(ap(o), c), [], [o])
+    def vts(o, i, s1, o1, s2=None, o2=None):
+        if o2 is None:
+            op("v", lambda: vec.tensor_scalar(ap(o), ap(i), s1, None, o1), [i], [o])
+        else:
+            op("v", lambda: vec.tensor_scalar(ap(o), ap(i), s1, s2, o1, o2), [i], [o])
+    def vtt(o, a, b, f): op("v", lambda: vec.tensor_tensor(ap(o), ap(a), ap(b), f), [a, b], [o])
+    def vgat(o, w, l): op("v", lambda: vec.tensor_copy(ap(o), ind(w, l)), [w, l], [o])
+    def vgtt(o, w, l, b, f): op("v", lambda: vec.tensor_tensor(ap(o), ind(w, l), ap(b), f), [w, l, b], [o])
+    def act(o, i, f=F.Copy, **k): op("s", lambda: sca.activation(ap(o), ap(i), f, **k), [i], [o])
+    def sgat(o, w, l): op("s", lambda: sca.activation(ap(o), ind(w, l), F.Copy), [w, l], [o])
+    def mm(o, w, i, start=True, stop=True): op("p", lambda: ten.matmul(ap(o), ap(w), ap(i), start, stop), [w, i], [o])
+
+    def rot(k, name="E2"):
+        a = 16 * (k % 8)
+        return (name, a, a + 128)
+
+    def transfer(srcs, dsts, ranks, engines, sem_arr):
+        ids = []
+        for r in ranks:
+            rid, pid = topo.addr(T.cores[r])[:2]
+            ids.append(DstId(rid=rid, pnc=pid))
+        return RemoteDMATransfer(srcs=[ap(s) for s in srcs], dsts=[ap(d) for d in dsts], dst_ids=ids,
+                                 dma_engine_mask=sum(1 << e for e in engines), remote_sem=T.sem[sem_arr])
+
+    def send(pairs, sem_arr, sem_loc):
+        tr, n = [], 0
+        for i, (r, s, d) in enumerate(pairs):
+            e = topo.engines(core, T.cores[r])
+            n = len(e) // 4
+            tr.append(transfer([s], [d], [r], e[n * i:n * i + n], sem_arr))
+
+        def call():
+            g.remote_dma_fused(tr, local_sem=T.sem[sem_loc])
+        op("g", call, [s for _, s, _ in pairs], [], sem_loc, len(pairs) * n)
+        return n
+
+    def send_all(src, sem_arr, sem_loc):
+        e = topo.engines(core, T.cores[others[0]])
+        tr = transfer([src], [src] * len(others), others, e, sem_arr)
+
+        def call():
+            g.remote_dma_fused([tr], local_sem=T.sem[sem_loc])
+        op("g", call, [src], [], sem_loc, len(e))
+        return len(e)
+
+    op("y", lambda: g.sync.dma_start(T.snI[:], T.sn[:]), [], [full("snI")], "dsn")
+    op("s", lambda: sca.dma_start(T.xb[:], T.x[:]), [], [full("xb")], "dx")
+    op("y", lambda: g.sync.dma_start(T.vlI[:], T.vl[:]), [], [full("vlI")], "dvl")
+    op("s", lambda: sca.dma_start(T.plI[:], T.pl[:]), [], [full("plI")], "dpl")
+    vset(full("ones"), 1.0)
+    op("g", lambda: g.iota(T.dg[:], [[-1, 16]], 112, 1), [], [full("dg")])
+    op("g", lambda: g.iota(T.kkI[:], [[1, 48]], 0, 0), [], [full("kkI")])
+    op("g", lambda: g.affine_select(T.E2[:], T.ones[:], [[0, 2], [-1, 128]], A.is_equal, 0.0, 0, 1), [full("ones")], [full("E2")])
+    op("g", lambda: g.affine_select(T.BO[:], T.ones[:, 0:128], [[-16, 8], [0, 16]], A.is_ge, 0.0, 0, 1), [("ones", 0, 128)], [full("BO")])
+    op("g", lambda: g.affine_select(T.BO2[:], T.BO[:], [[16, 8], [0, 16]], A.is_ge, 0.0, 15, -1), [full("BO")], [full("BO2")])
+    vts(full("dg2"), full("dg"), 15, A.bitwise_and)
+    vcopy(full("kk16"), full("kkI"))
+    vts(("mask", 0, 16), full("dg2"), 0, A.is_equal)
+    vset(("seg", 0, 16), 1.0)
+    vset(("seg", 0, 1), 0.0)
+
+    def widen(name, copy):
+        w = 16
+        while w < E:
+            n = min(w, E - w)
+            copy((name, w, w + n), (name, 0, n))
+            w += n
+
+    def zeros(name, base):
+        for k in range(N):
+            act((name, base + k * CAP, base + k * CAP + CAP), ("ones", 0, CAP), F.Copy, scale=0.0)
+    widen("mask", vcopy)
+    zeros("QS", 0)
+    act(full("E2f"), full("E2"))
+    act(full("BOf"), full("BO2"))
+
+    vcopy(full("sn16"), full("snI"))
+    def snl(q): return ("sn16", 14 * q, 14 * q + 14)
+    vgat(blk("XS", others[0]), full("xb"), snl(others[0]))
+    sgat(blk("XS", others[1]), full("xb"), snl(others[1]))
+    sgat(blk("XS", others[2]), full("xb"), snl(others[2]))
+    n = send([(q, blk("XS", q), blk("XW", me)) for q in others], "ax%d" % me, "lx")
+    for p in others:
+        arrive("ax%d" % p, n, blk("XW", p))
+    sgat(blk("XW", me), full("xb"), snl(me))
+
+    vts(full("vt"), full("vlI"), 1024.0, A.mult)
+    vcopy(full("vl16"), full("vlI"))
+    for d in range(3):
+        a, b = (d + 1) % 3, (d + 2) % 3
+        vtt(("Qw", 16 * d, 16 * d + 16), ("vt", 16 * a, 16 * a + 16), ("vlI", 16 * b, 16 * b + 16), A.add)
+    for h in range(2):
+        vgtt(("QB", H * h, H * h + H), full("Qw"), ("kk16", 24 * h, 24 * h + 24), ("mask", H * h, H * h + H), A.mult)
+        mm(("b%d" % (6 + h), 0, H), full("BOf"), ("QB", H * h, H * h + H))
+        act(("QF", H * h, H * h + H), ("b%d" % (6 + h), 0, H))
+    vcopy(full("pl16"), full("plI"))
+    widen("seg", act)
+    own = (me * S4, me * S4 + S4)
+    vset(("W1",) + own, 0.0)
+    k1, k2, k3 = full("k1"), full("k2"), full("k3")
+    for i, k in ((1, k1), (2, k2), (3, k3)):
+        vts(k, full("plI"), CAP * i, A.is_ge, float(CAP), A.mult)
+    vtt(k1, k1, k2, A.add)
+    for h in range(2):
+        vtt(("pp", 48 * h, 48 * h + 48), k1, k3, A.add)
+    for h in range(2):
+        i, o, l = ("QF", H * h, H * h + H), full("QS"), ("vl16", 24 * h, 24 * h + 24)
+        op("v", lambda: vec.tensor_copy(ind(o, l), ap(i)), [i, l], [o])
+    n = send([(q, blk("QS", q), blk("QW", me)) for q in others], "aq%d" % me, "lq")
+    for p in others:
+        arrive("aq%d" % p, n, blk("QW", p))
+
+    def turn(win, base, ks, banks, evac, src={}, ident="E2"):
+        for grp, bank, q in zip([[1, 2], [3]], banks, evac):
+            for i, p in enumerate(grp):
+                s = src.get(p, (win, base + p * CAP, base + p * CAP + CAP))
+                mm((bank, i * CAP, i * CAP + CAP), rot(ks[p], ident), s)
+            o = (win, base + grp[0] * CAP, base + grp[-1] * CAP + CAP)
+            i = (bank, 0, CAP * len(grp))
+            if q == "v":
+                vcopy(o, i)
+            else:
+                act(o, i)
+
+    if me:
+        turn("XW", 0, [-p * me for p in range(N)], ["b0", "b1"], "vs")
+
+    def plh(h): return ("pl16", 24 * h, 24 * h + 24)
+    def check(t, mA, mB, out, base):
+        u = str(t)
+        sA, sB = ("s" + u, 0, H), ("s" + u, H, E)
+        aA, aB, pB, nA = full("aA" + u), full("aB" + u), ("b1", 0, H), ("b0", 0, H)
+        vts(nA, mA, -1.0, A.mult)
+        act(sB, mB, F.Sign, bias=0.5)
+        vtt(aA, mA, nA, A.max)
+        act(sA, mA, F.Sign, bias=0.5)
+        act(pB, mB, F.Abs)
+        for e in range(6):
+            mm(("b4", 0, M), rot(0), ("s" + u, e * M, e * M + M), e == 0, e == 5)
+        act(aB, mB, F.Abs)
+        L0, L1, L01, L2 = ("L" + u, 0, 128), ("L" + u, 128, 256), ("L" + u, 0, 256), ("b3", H, 512)
+        vtt(L01, ("aA" + u, 0, 256), ("b1", 0, 256), A.min)
+        vtt(L2, ("aA" + u, 256, H), ("b1", 256, H), A.min)
+        f1, f2, f3 = full("f1_" + u), full("f2_" + u), full("f3_" + u)
+        act(f1, ("b4", 0, M), F.Abs)
+        vtt(("b3", 256, 384), L0, L1, A.min)
+        vtt(("b3", 0, 128), L1, L2, A.min)
+        vtt(("b3", 128, 256), L0, L2, A.min)
+        act(f2, f1, F.Abs, bias=-4.0)
+        act(f3, f2, F.Abs, bias=-2.0)
+        for i in range(3):
+            act(("b5", i * M, i * M + M), f3, F.Identity, scale=-1.0, bias=1.0)
+        vtt(("mg" + u, H, E), aA, ("b3", 0, H), A.min)
+        vtt(("mg" + u, 0, H), aB, ("b3", 0, H), A.min)
+        for h, s in ((0, sA), (1, sB)):
+            vtt(("z" + u, H * h, H * h + H), s, ("b5", 0, H), A.mult)
+        o, l = (out, base, base + S4), full("pl16")
+        op("v", lambda: vec.tensor_tensor(ind(o, l), ap(full("z" + u)), ap(full("mg" + u)), A.mult),
+           [full("z" + u), full("mg" + u), l], [o])
+
+    vgat(("xe", 0, H), full("XW"), plh(0))
+    sgat(("xe", H, E), full("XW"), plh(1))
+    check(1, ("xe", 0, H), ("xe", H, E), "W1", me * S4)
+    n = send_all(("W1",) + own, "a1_%d" % me, "l1")
+    for q in others:
+        arrive("a1_%d" % q, n, ("W1", q * S4, q * S4 + S4))
+
+    if me:
+        turn("QW", 0, [-p * me for p in range(N)], ["b6", "b7"], "ss", {me: blk("QS", me)}, "E2f")
+    else:
+        act(blk("QW", 0), blk("QS", 0))
+    zeros("W2", me * S4)
+    vgtt(full("QG"), full("QW"), full("pl16"), full("mask"), A.mult)
+    op("v", lambda: vec.tensor_tensor_scan(T.QC[:], T.seg[:], T.QG[:], 0.0, A.mult, A.add), [full("seg"), full("QG")], [full("QC")])
+    op("v", lambda: vec.tensor_copy(T.qi[:], T.QC[:, 15:E:16]), [full("QC")], [full("qi")])
+    vts(("ee", 0, 48), full("qi"), 10, A.logical_shift_right)
+    vts(("ee", 48, 96), full("qi"), 1023, A.bitwise_and)
+    g1, g2, g3, g4 = full("g1"), full("g2"), full("g3"), full("g4")
+    for i, k in ((1, g1), (2, g2), (3, g3)):
+        vts(k, full("ee"), CAP * i, A.is_ge, float(S4 - CAP), A.mult)
+    vtt(g4, full("ee"), full("pp"), A.add)
+    vtt(g1, g1, g2, A.add)
+    vtt(g3, g3, g4, A.add)
+    vtt(g2, g1, g3, A.add)
+    vcopy(full("LL"), g2)
+
+    for t, win in ((2, "W1"), (3, "W2")):
+        u = str(t)
+        for i, (q, ev) in enumerate(zip(others, ("vs", "vs", "sv"))):
+            turn(win, q * S4, [-p * (me - q) for p in range(N)], ["b%d" % (2 * i), "b%d" % (2 * i + 1)], ev)
+        for h in range(2):
+            hh = (H * h, H * h + H)
+            vgtt(("t" + u,) + hh, full(win), ("LL", 24 * h, 24 * h + 24), ("xe",) + hh, A.add)
+            sgat(("r" + u,) + hh, full(win), ("LL", 48 + 24 * h, 72 + 24 * h))
+            mm(("b%d" % (6 + h), 0, H), rot(0), ("t" + u,) + hh, True, False)
+            mm(("b%d" % (6 + h), 0, H), rot(0), ("r" + u,) + hh, False, True)
+        vts(full("c" + u), ("b6", 0, H), 63.0, A.min, -63.0, A.max)
+        if t == 2:
+            check(t, full("c2"), ("b7", 0, H), "W2", me * S4)
+            n = send_all(("W2",) + own, "a2_%d" % me, "l2")
+            for q in others:
+                arrive("a2_%d" % q, n, ("W2", q * S4, q * S4 + S4))
+            zeros("R3", 0)
+        else:
+            check(t, full("c3"), ("b7", 0, H), "R3", 0)
+            n = send([(p, blk("R3", p), blk("VW", me)) for p in others], "a3_%d" % me, "l3")
+            for q in others:
+                arrive("a3_%d" % q, n, blk("VW", q))
+
+    if me:
+        turn("VW", 0, [q * me for q in range(N)], ["b0", "b1"], "vs", {me: blk("R3", me)})
+    else:
+        vcopy(blk("VW", 0), blk("R3", 0))
+    y0, y1 = ("yt", 0, V), ("yt", V, 2 * V)
+    vgtt(y0, full("VW"), ("vl16", 0, 16), full("xb"), A.add)
+    sgat(y1, full("VW"), ("vl16", 16, 32))
+    vgat(("yt", 512, 640), full("VW"), ("vl16", 32, 40))
+    sgat(("yt", 640, 768), full("VW"), ("vl16", 40, 48))
+    for h in range(2):
+        for d in range(3):
+            mm(("b%d" % (2 + h), 0, 128), rot(0), ("yt", d * V + 128 * h, d * V + 128 * h + 128), d == 0, d == 2)
+    vcopy(("yo", 0, 128), ("b2", 0, 128))
+    act(("yo", 128, 256), ("b3", 0, 128))
+    op("y", lambda: g.sync.dma_start(T.y[:, 0:128], T.yo[:, 0:128]), [("yo", 0, 128)], [], "dy0")
+    op("s", lambda: sca.dma_start(T.y[:, 128:256], T.yo[:, 128:256]), [("yo", 128, 256)], [], "dy1")
+    finish()

@@ -2,7 +2,7 @@ import numpy as np
 from concourse.bass import DstId, RemoteDMATransfer
 from concourse.mybir import AluOpType as A, ActivationFunctionType as F
 
-N, V, M, CAP = 4, 256, 128, 224
+N, V, M, CAP, B = 4, 256, 128, 224, 63
 E = 768
 S4 = N * CAP
 H = E // 2
@@ -12,6 +12,7 @@ SCRATCH = {
     "sn16": ("sbuf", [128, 56], "uint16"), "pl16": ("sbuf", [128, 48], "uint16"), "vl16": ("sbuf", [128, 48], "uint16"),
     "ones": ("sbuf", [128, 256], "bfloat16"), "E2": ("sbuf", [128, 256], "bfloat16"), "E2f": ("sbuf", [128, 256], "float32"),
     "BO": ("sbuf", [128, 128], "bfloat16"), "BO2": ("sbuf", [128, 128], "bfloat16"), "BOf": ("sbuf", [128, 128], "float32"),
+    "I2": ("sbuf", [128, 128], "bfloat16"), "sz": ("sbuf", [128, 48], "bfloat16"),
     "kkI": ("sbuf", [128, 48], "int32"), "kk16": ("sbuf", [128, 48], "uint16"),
     "dg": ("sbuf", [128, 16], "int32"), "dg2": ("sbuf", [128, 16], "int32"),
     "mask": ("sbuf", [128, E], "bfloat16"), "seg": ("sbuf", [128, E], "bfloat16"),
@@ -19,16 +20,14 @@ SCRATCH = {
     "vt": ("sbuf", [128, 48], "float32"), "Qw": ("sbuf", [128, 48], "float32"), "QB": ("sbuf", [128, E], "float32"),
     "QF": ("sbuf", [128, E], "float32"), "QS": ("sbuf", [128, S4], "float32"), "QW": ("sbuf", [128, S4], "float32"),
     "QG": ("sbuf", [128, E], "float32"), "QC": ("sbuf", [128, E], "float32"), "qi": ("sbuf", [128, 48], "int32"),
-    "ee": ("sbuf", [128, 96], "int32"), "g1": ("sbuf", [128, 96], "float32"), "g2": ("sbuf", [128, 96], "float32"),
-    "g3": ("sbuf", [128, 96], "float32"), "g4": ("sbuf", [128, 96], "float32"), "LL": ("sbuf", [128, 96], "uint16"),
-    "k1": ("sbuf", [128, 48], "float32"), "k2": ("sbuf", [128, 48], "float32"), "k3": ("sbuf", [128, 48], "float32"),
-    "pp": ("sbuf", [128, 96], "float32"),
+    "ee": ("sbuf", [128, 96], "int32"), "LL": ("sbuf", [128, 96], "uint16"), "vi": ("sbuf", [128, 48], "int32"),
+    "vq": ("sbuf", [128, 48], "float32"), "vq2": ("sbuf", [128, 48], "float32"), "vp": ("sbuf", [128, 48], "float32"),
     "W1": ("sbuf", [128, N * S4], "bfloat16"), "W2": ("sbuf", [128, N * S4], "bfloat16"),
     "R3": ("sbuf", [128, S4], "bfloat16"), "VW": ("sbuf", [128, S4], "bfloat16"),
     "yt": ("sbuf", [128, E], "bfloat16"), "yo": ("sbuf", [128, V], "float32"),
 }
 for _t in "123":
-    for _n, _w in (("t", E), ("r", E), ("c", H), ("s", E), ("aA", H), ("aB", H), ("L", 256), ("z", E), ("mg", E)):
+    for _n, _w in (("t", H), ("m", H), ("r", E), ("n", E), ("s", E), ("aA", H), ("aB", H), ("L", 256), ("z", E), ("mg", E)):
         SCRATCH[_n + _t] = ("sbuf", [128, _w], "bfloat16")
     for _n in ("f1", "f2", "f3"):
         SCRATCH[_n + "_" + _t] = ("sbuf", [128, M], "bfloat16")
@@ -166,6 +165,19 @@ def rank_program(g, core, T, topo):
         op("g", call, [src], [], sem_loc, len(e))
         return len(e)
 
+    def widen(name, copy):
+        w, steps = 16, []
+        while w < E:
+            n = min(w, E - w)
+            steps.append(lambda w=w, n=n: copy((name, w, w + n), (name, 0, n)))
+            w += n
+        return steps
+
+    def zeros(name, base):
+        for k in range(N):
+            act((name, base + k * CAP, base + k * CAP + CAP), ("ones", 0, CAP), F.Copy, scale=0.0)
+
+    own = (me * S4, me * S4 + S4)
     op("y", lambda: g.sync.dma_start(T.snI[:], T.sn[:]), [], [full("snI")], "dsn")
     op("s", lambda: sca.dma_start(T.xb[:], T.x[:]), [], [full("xb")], "dx")
     op("y", lambda: g.sync.dma_start(T.vlI[:], T.vl[:]), [], [full("vlI")], "dvl")
@@ -179,56 +191,53 @@ def rank_program(g, core, T, topo):
     vts(full("dg2"), full("dg"), 15, A.bitwise_and)
     vcopy(full("kk16"), full("kkI"))
     vts(("mask", 0, 16), full("dg2"), 0, A.is_equal)
-    vset(("seg", 0, 16), 1.0)
-    vset(("seg", 0, 1), 0.0)
-
-    def widen(name, copy):
-        w = 16
-        while w < E:
-            n = min(w, E - w)
-            copy((name, w, w + n), (name, 0, n))
-            w += n
-
-    def zeros(name, base):
-        for k in range(N):
-            act((name, base + k * CAP, base + k * CAP + CAP), ("ones", 0, CAP), F.Copy, scale=0.0)
-    widen("mask", vcopy)
+    vset(full("sz"), 0.0)
+    vset(("W1",) + own, 0.0)
     zeros("QS", 0)
-    act(full("E2f"), full("E2"))
-    act(full("BOf"), full("BO2"))
+    mask = widen("mask", vcopy)
+    mask[0]()
+    mask[1]()
 
     vcopy(full("sn16"), full("snI"))
-    def snl(q): return ("sn16", 14 * q, 14 * q + 14)
-    vgat(blk("XS", others[0]), full("xb"), snl(others[0]))
-    sgat(blk("XS", others[1]), full("xb"), snl(others[1]))
-    sgat(blk("XS", others[2]), full("xb"), snl(others[2]))
+    def snl(q, lo=0, hi=14): return ("sn16", 14 * q + lo, 14 * q + hi)
+    q0, q1, q2 = others
+    vgat(blk("XS", q0), full("xb"), snl(q0))
+    sgat(blk("XS", q1), full("xb"), snl(q1))
+    vgat(("XS", q2 * CAP, q2 * CAP + 96), full("xb"), snl(q2, 0, 6))
+    sgat(("XS", q2 * CAP + 96, q2 * CAP + CAP), full("xb"), snl(q2, 6, 14))
     n = send([(q, blk("XS", q), blk("XW", me)) for q in others], "ax%d" % me, "lx")
     for p in others:
         arrive("ax%d" % p, n, blk("XW", p))
+    act(full("BOf"), full("BO2"))
     sgat(blk("XW", me), full("xb"), snl(me))
+    act(full("E2f"), full("E2"))
+    act(full("I2"), ("E2", 0, 128), F.Copy, scale=2.0)
 
-    vts(full("vt"), full("vlI"), 1024.0, A.mult)
+    vts(full("vq"), full("vlI"), 111.5, A.subtract, 1.0 / CAP, A.mult)
+    mask[2]()
+    vcopy(full("vi"), full("vq"))
+    mask[3]()
+    vts(full("vq2"), full("vi"), float(S4 - CAP), A.mult)
     vcopy(full("vl16"), full("vlI"))
+    vtt(full("vp"), full("vlI"), full("vq2"), A.add)
+    mask[4]()
+    vts(full("vt"), full("vp"), 4096.0, A.mult, 4097.0 * CAP * me, A.add)
+    mask[5]()
     for d in range(3):
         a, b = (d + 1) % 3, (d + 2) % 3
-        vtt(("Qw", 16 * d, 16 * d + 16), ("vt", 16 * a, 16 * a + 16), ("vlI", 16 * b, 16 * b + 16), A.add)
-    for h in range(2):
-        vgtt(("QB", H * h, H * h + H), full("Qw"), ("kk16", 24 * h, 24 * h + 24), ("mask", H * h, H * h + H), A.mult)
-        mm(("b%d" % (6 + h), 0, H), full("BOf"), ("QB", H * h, H * h + H))
-        act(("QF", H * h, H * h + H), ("b%d" % (6 + h), 0, H))
-    vcopy(full("pl16"), full("plI"))
-    widen("seg", act)
-    own = (me * S4, me * S4 + S4)
-    vset(("W1",) + own, 0.0)
-    k1, k2, k3 = full("k1"), full("k2"), full("k3")
-    for i, k in ((1, k1), (2, k2), (3, k3)):
-        vts(k, full("plI"), CAP * i, A.is_ge, float(CAP), A.mult)
-    vtt(k1, k1, k2, A.add)
-    for h in range(2):
-        vtt(("pp", 48 * h, 48 * h + 48), k1, k3, A.add)
-    for h in range(2):
-        i, o, l = ("QF", H * h, H * h + H), full("QS"), ("vl16", 24 * h, 24 * h + 24)
+        vtt(("Qw", 16 * d, 16 * d + 16), ("vt", 16 * a, 16 * a + 16), ("vp", 16 * b, 16 * b + 16), A.add)
+    for d in range(3):
+        dd = (V * d, V * d + V)
+        vgtt(("QB",) + dd, full("Qw"), ("kk16", 16 * d, 16 * d + 16), ("mask",) + dd, A.mult)
+        mm(("b%d" % (5 + d), 0, V), full("BOf"), ("QB",) + dd)
+        act(("QF",) + dd, ("b%d" % (5 + d), 0, V))
+    vset(full("seg"), 1.0)
+    op("v", lambda: vec.tensor_copy(T.seg[:, 0:E:16], T.sz[:]), [full("sz")], [full("seg")])
+    for d in range(3):
+        i, o, l = ("QF", V * d, V * d + V), full("QS"), ("vl16", 16 * d, 16 * d + 16)
         op("v", lambda: vec.tensor_copy(ind(o, l), ap(i)), [i, l], [o])
+        if d == 0:
+            vcopy(full("pl16"), full("plI"))
     n = send([(q, blk("QS", q), blk("QW", me)) for q in others], "aq%d" % me, "lq")
     for p in others:
         arrive("aq%d" % p, n, blk("QW", p))
@@ -249,23 +258,24 @@ def rank_program(g, core, T, topo):
         turn("XW", 0, [-p * me for p in range(N)], ["b0", "b1"], "vs")
 
     def plh(h): return ("pl16", 24 * h, 24 * h + 24)
-    def check(t, mA, mB, out, base):
+    def check(t, mA, mB, mB2, out, base):
         u = str(t)
-        sA, sB = ("s" + u, 0, H), ("s" + u, H, E)
-        aA, aB, pB, nA = full("aA" + u), full("aB" + u), ("b1", 0, H), ("b0", 0, H)
-        vts(nA, mA, -1.0, A.mult)
-        act(sB, mB, F.Sign, bias=0.5)
-        vtt(aA, mA, nA, A.max)
-        act(sA, mA, F.Sign, bias=0.5)
+        s, n = full("s" + u), full("n" + u)
+        aA, aB, pB = full("aA" + u), full("aB" + u), ("b1", 0, H)
+        act(aA, mA, F.Abs)
         act(pB, mB, F.Abs)
+        vts(("n" + u, 0, H), mA, 0.0, A.is_ge)
+        vts(("n" + u, H, E), mB2, 0.0, A.is_ge)
+        if t > 1:
+            vts(aA, aA, float(B), A.min)
         for e in range(6):
-            mm(("b4", 0, M), rot(0), ("s" + u, e * M, e * M + M), e == 0, e == 5)
+            mm(("b4", 0, M), full("I2"), ("n" + u, e * M, e * M + M), e == 0, e == 5)
         act(aB, mB, F.Abs)
         L0, L1, L01, L2 = ("L" + u, 0, 128), ("L" + u, 128, 256), ("L" + u, 0, 256), ("b3", H, 512)
         vtt(L01, ("aA" + u, 0, 256), ("b1", 0, 256), A.min)
         vtt(L2, ("aA" + u, 256, H), ("b1", 256, H), A.min)
         f1, f2, f3 = full("f1_" + u), full("f2_" + u), full("f3_" + u)
-        act(f1, ("b4", 0, M), F.Abs)
+        act(f1, ("b4", 0, M), F.Abs, bias=-6.0)
         vtt(("b3", 256, 384), L0, L1, A.min)
         vtt(("b3", 0, 128), L1, L2, A.min)
         vtt(("b3", 128, 256), L0, L2, A.min)
@@ -273,17 +283,18 @@ def rank_program(g, core, T, topo):
         act(f3, f2, F.Abs, bias=-2.0)
         for i in range(3):
             act(("b5", i * M, i * M + M), f3, F.Identity, scale=-1.0, bias=1.0)
+        vts(s, n, 2.0, A.mult, 1.0, A.subtract)
         vtt(("mg" + u, H, E), aA, ("b3", 0, H), A.min)
         vtt(("mg" + u, 0, H), aB, ("b3", 0, H), A.min)
-        for h, s in ((0, sA), (1, sB)):
-            vtt(("z" + u, H * h, H * h + H), s, ("b5", 0, H), A.mult)
+        for lo, hi in ((0, H), (H, E)):
+            vtt(("z" + u, lo, hi), ("s" + u, lo, hi), ("b5", 0, H), A.mult)
         o, l = (out, base, base + S4), full("pl16")
         op("v", lambda: vec.tensor_tensor(ind(o, l), ap(full("z" + u)), ap(full("mg" + u)), A.mult),
            [full("z" + u), full("mg" + u), l], [o])
 
     vgat(("xe", 0, H), full("XW"), plh(0))
     sgat(("xe", H, E), full("XW"), plh(1))
-    check(1, ("xe", 0, H), ("xe", H, E), "W1", me * S4)
+    check(1, ("xe", 0, H), ("xe", H, E), ("xe", H, E), "W1", me * S4)
     n = send_all(("W1",) + own, "a1_%d" % me, "l1")
     for q in others:
         arrive("a1_%d" % q, n, ("W1", q * S4, q * S4 + S4))
@@ -293,39 +304,46 @@ def rank_program(g, core, T, topo):
     else:
         act(blk("QW", 0), blk("QS", 0))
     zeros("W2", me * S4)
-    vgtt(full("QG"), full("QW"), full("pl16"), full("mask"), A.mult)
-    op("v", lambda: vec.tensor_tensor_scan(T.QC[:], T.seg[:], T.QG[:], 0.0, A.mult, A.add), [full("seg"), full("QG")], [full("QC")])
-    op("v", lambda: vec.tensor_copy(T.qi[:], T.QC[:, 15:E:16]), [full("QC")], [full("qi")])
-    vts(("ee", 0, 48), full("qi"), 10, A.logical_shift_right)
-    vts(("ee", 48, 96), full("qi"), 1023, A.bitwise_and)
-    g1, g2, g3, g4 = full("g1"), full("g2"), full("g3"), full("g4")
-    for i, k in ((1, g1), (2, g2), (3, g3)):
-        vts(k, full("ee"), CAP * i, A.is_ge, float(S4 - CAP), A.mult)
-    vtt(g4, full("ee"), full("pp"), A.add)
-    vtt(g1, g1, g2, A.add)
-    vtt(g3, g3, g4, A.add)
-    vtt(g2, g1, g3, A.add)
-    vcopy(full("LL"), g2)
+    hs = [(H * h, H * h + H) for h in range(2)]
+    for h in range(2):
+        vgtt(("QG",) + hs[h], full("QW"), plh(h), ("mask",) + hs[h], A.mult)
+    for lo, hi in hs:
+        op("v", lambda: vec.tensor_tensor_scan(T.QC[:, lo:hi], T.seg[:, lo:hi], T.QG[:, lo:hi], 0.0, A.mult, A.add),
+           [("seg", lo, hi), ("QG", lo, hi)], [("QC", lo, hi)])
+    for lo, hi in hs:
+        op("v", lambda: vec.tensor_copy(T.qi[:, lo // 16:hi // 16], T.QC[:, lo + 15:hi:16]), [("QC", lo, hi)], [("qi", lo // 16, hi // 16)])
+    for c, k, f in ((0, 12, A.logical_shift_right), (48, 4095, A.bitwise_and)):
+        for h in range(2):
+            vts(("ee", c + 24 * h, c + 24 * h + 24), ("qi", 24 * h, 24 * h + 24), k, f)
+    for c in (0, 48):
+        vcopy(("LL", c, c + 48), ("ee", c, c + 48))
 
     for t, win in ((2, "W1"), (3, "W2")):
         u = str(t)
         for i, (q, ev) in enumerate(zip(others, ("vs", "vs", "sv"))):
             turn(win, q * S4, [-p * (me - q) for p in range(N)], ["b%d" % (2 * i), "b%d" % (2 * i + 1)], ev)
-        for h in range(2):
-            hh = (H * h, H * h + H)
-            vgtt(("t" + u,) + hh, full(win), ("LL", 24 * h, 24 * h + 24), ("xe",) + hh, A.add)
-            sgat(("r" + u,) + hh, full(win), ("LL", 48 + 24 * h, 72 + 24 * h))
-            mm(("b%d" % (6 + h), 0, H), rot(0), ("t" + u,) + hh, True, False)
-            mm(("b%d" % (6 + h), 0, H), rot(0), ("r" + u,) + hh, False, True)
-        vts(full("c" + u), ("b6", 0, H), 63.0, A.min, -63.0, A.max)
+        mA, rB1, rB2, mB, mB2 = full("m" + u), ("r" + u, 0, H), ("r" + u, H, E), ("b7", 0, H), ("b6", 0, H)
+        pieces = ((0, H // 2), (H // 2, H))
+        for o in (mB, mB2):
+            mm(o, rot(0), ("xe", H, E), True, False)
+        for lo, hi in pieces:
+            vgtt(("t" + u, lo, hi), full(win), ("LL", lo // 16, hi // 16), ("xe", lo, hi), A.add)
+        sgat(rB1, full(win), ("LL", 24, 48))
+        for o in (mB, mB2):
+            mm(o, rot(0), rB1, False, False)
+        for lo, hi in pieces:
+            vgtt(("m" + u, lo, hi), full(win), ("LL", 48 + lo // 16, 48 + hi // 16), ("t" + u, lo, hi), A.add)
+        sgat(rB2, full(win), ("LL", 72, 96))
+        for o in (mB, mB2):
+            mm(o, rot(0), rB2, False, True)
         if t == 2:
-            check(t, full("c2"), ("b7", 0, H), "W2", me * S4)
+            check(t, mA, mB, mB2, "W2", me * S4)
             n = send_all(("W2",) + own, "a2_%d" % me, "l2")
             for q in others:
                 arrive("a2_%d" % q, n, ("W2", q * S4, q * S4 + S4))
             zeros("R3", 0)
         else:
-            check(t, full("c3"), ("b7", 0, H), "R3", 0)
+            check(t, mA, mB, mB2, "R3", 0)
             n = send([(p, blk("R3", p), blk("VW", me)) for p in others], "a3_%d" % me, "l3")
             for q in others:
                 arrive("a3_%d" % q, n, blk("VW", q))
@@ -334,16 +352,11 @@ def rank_program(g, core, T, topo):
         turn("VW", 0, [q * me for q in range(N)], ["b0", "b1"], "vs", {me: blk("R3", me)})
     else:
         vcopy(blk("VW", 0), blk("R3", 0))
-    y0, y1 = ("yt", 0, V), ("yt", V, 2 * V)
-    vgtt(y0, full("VW"), ("vl16", 0, 16), full("xb"), A.add)
-    sgat(y1, full("VW"), ("vl16", 16, 32))
-    vgat(("yt", 512, 640), full("VW"), ("vl16", 32, 40))
-    sgat(("yt", 640, 768), full("VW"), ("vl16", 40, 48))
-    for h in range(2):
-        for d in range(3):
-            mm(("b%d" % (2 + h), 0, 128), rot(0), ("yt", d * V + 128 * h, d * V + 128 * h + 128), d == 0, d == 2)
-    vcopy(("yo", 0, 128), ("b2", 0, 128))
-    act(("yo", 128, 256), ("b3", 0, 128))
+    vgtt(("yt", 0, V), full("VW"), ("vl16", 0, 16), full("xb"), A.add)
+    sgat(("yt", 2 * V, 3 * V), full("VW"), ("vl16", 32, 48))
+    vgtt(("yt", V, 2 * V), full("VW"), ("vl16", 16, 32), ("yt", 0, V), A.add)
+    for lo, hi in ((0, 128), (128, 256)):
+        vtt(("yo", lo, hi), ("yt", V + lo, V + hi), ("yt", 2 * V + lo, 2 * V + hi), A.add)
     op("y", lambda: g.sync.dma_start(T.y[:, 0:128], T.yo[:, 0:128]), [("yo", 0, 128)], [], "dy0")
     op("s", lambda: sca.dma_start(T.y[:, 128:256], T.yo[:, 128:256]), [("yo", 128, 256)], [], "dy1")
     finish()

@@ -27,7 +27,7 @@ SCRATCH = {
     "yt": ("sbuf", [128, E], "bfloat16"), "yo": ("sbuf", [128, V], "float32"),
 }
 for _t in "123":
-    for _n, _w in (("t", H), ("m", H), ("r", E), ("n", E), ("s", E), ("aA", H), ("aB", H), ("L", 256), ("z", E), ("mg", E)):
+    for _n, _w in (("t", H), ("m", H), ("r", E), ("n", E), ("aA", H), ("aB", H), ("L", 256), ("z", E), ("mg", E)):
         SCRATCH[_n + _t] = ("sbuf", [128, _w], "bfloat16")
     for _n in ("f1", "f2", "f3"):
         SCRATCH[_n + "_" + _t] = ("sbuf", [128, M], "bfloat16")
@@ -232,12 +232,13 @@ def rank_program(g, core, T, topo):
         mm(("b%d" % (5 + d), 0, V), full("BOf"), ("QB",) + dd)
         act(("QF",) + dd, ("b%d" % (5 + d), 0, V))
     vset(full("seg"), 1.0)
-    op("v", lambda: vec.tensor_copy(T.seg[:, 0:E:16], T.sz[:]), [full("sz")], [full("seg")])
     for d in range(3):
         i, o, l = ("QF", V * d, V * d + V), full("QS"), ("vl16", 16 * d, 16 * d + 16)
         op("v", lambda: vec.tensor_copy(ind(o, l), ap(i)), [i, l], [o])
         if d == 0:
             vcopy(full("pl16"), full("plI"))
+        elif d == 1:
+            op("v", lambda: vec.tensor_copy(T.seg[:, 0:E:16], T.sz[:]), [full("sz")], [full("seg")])
     n = send([(q, blk("QS", q), blk("QW", me)) for q in others], "aq%d" % me, "lq")
     for p in others:
         arrive("aq%d" % p, n, blk("QW", p))
@@ -255,39 +256,40 @@ def rank_program(g, core, T, topo):
                 act(o, i)
 
     if me:
-        turn("XW", 0, [-p * me for p in range(N)], ["b0", "b1"], "vs")
+        turn("XW", 0, [-p * me for p in range(N)], ["b0", "b1"], "sv")
 
+    pieces = ((0, H // 2), (H // 2, H))
     def plh(h): return ("pl16", 24 * h, 24 * h + 24)
     def check(t, mA, mB, mB2, out, base):
         u = str(t)
-        s, n = full("s" + u), full("n" + u)
         aA, aB, pB = full("aA" + u), full("aB" + u), ("b1", 0, H)
-        act(aA, mA, F.Abs)
-        act(pB, mB, F.Abs)
-        vts(("n" + u, 0, H), mA, 0.0, A.is_ge)
-        vts(("n" + u, H, E), mB2, 0.0, A.is_ge)
+        act(aA, mA, F.Abs, scale=4.0)
+        act(pB, mB, F.Abs, scale=4.0)
+        for lo, hi in pieces:
+            vts(("n" + u, lo, hi), (mA[0], lo, hi), 0.0, A.is_ge, 0.5, A.subtract)
+        vts(("n" + u, H, E), mB2, 0.0, A.is_ge, 0.5, A.subtract)
         if t > 1:
-            vts(aA, aA, float(B), A.min)
+            vts(aA, aA, 4.0 * B, A.min)
         for e in range(6):
             mm(("b4", 0, M), full("I2"), ("n" + u, e * M, e * M + M), e == 0, e == 5)
-        act(aB, mB, F.Abs)
+        act(aB, mB, F.Abs, scale=4.0)
         L0, L1, L01, L2 = ("L" + u, 0, 128), ("L" + u, 128, 256), ("L" + u, 0, 256), ("b3", H, 512)
         vtt(L01, ("aA" + u, 0, 256), ("b1", 0, 256), A.min)
         vtt(L2, ("aA" + u, 256, H), ("b1", 256, H), A.min)
         f1, f2, f3 = full("f1_" + u), full("f2_" + u), full("f3_" + u)
-        act(f1, ("b4", 0, M), F.Abs, bias=-6.0)
+        act(f1, ("b4", 0, M), F.Abs)
         vtt(("b3", 256, 384), L0, L1, A.min)
         vtt(("b3", 0, 128), L1, L2, A.min)
         vtt(("b3", 128, 256), L0, L2, A.min)
         act(f2, f1, F.Abs, bias=-4.0)
-        act(f3, f2, F.Abs, bias=-2.0)
+        vts(f3, f2, 2.0, A.is_equal, 0.5, A.subtract)
         for i in range(3):
-            act(("b5", i * M, i * M + M), f3, F.Identity, scale=-1.0, bias=1.0)
-        vts(s, n, 2.0, A.mult, 1.0, A.subtract)
-        vtt(("mg" + u, H, E), aA, ("b3", 0, H), A.min)
+            mm(("b5", i * M, i * M + M), rot(0), f3)
+        for lo, hi in ((256, H), (0, 256)):
+            vtt(("mg" + u, H + lo, H + hi), ("aA" + u, lo, hi), ("b3", lo, hi), A.min)
         vtt(("mg" + u, 0, H), aB, ("b3", 0, H), A.min)
         for lo, hi in ((0, H), (H, E)):
-            vtt(("z" + u, lo, hi), ("s" + u, lo, hi), ("b5", 0, H), A.mult)
+            vtt(("z" + u, lo, hi), ("n" + u, lo, hi), ("b5", 0, H), A.mult)
         o, l = (out, base, base + S4), full("pl16")
         op("v", lambda: vec.tensor_tensor(ind(o, l), ap(full("z" + u)), ap(full("mg" + u)), A.mult),
            [full("z" + u), full("mg" + u), l], [o])
@@ -323,18 +325,17 @@ def rank_program(g, core, T, topo):
         for i, (q, ev) in enumerate(zip(others, ("vs", "vs", "sv"))):
             turn(win, q * S4, [-p * (me - q) for p in range(N)], ["b%d" % (2 * i), "b%d" % (2 * i + 1)], ev)
         mA, rB1, rB2, mB, mB2 = full("m" + u), ("r" + u, 0, H), ("r" + u, H, E), ("b7", 0, H), ("b6", 0, H)
-        pieces = ((0, H // 2), (H // 2, H))
-        for o in (mB, mB2):
+        for o in (mB2, mB):
             mm(o, rot(0), ("xe", H, E), True, False)
         for lo, hi in pieces:
             vgtt(("t" + u, lo, hi), full(win), ("LL", lo // 16, hi // 16), ("xe", lo, hi), A.add)
         sgat(rB1, full(win), ("LL", 24, 48))
-        for o in (mB, mB2):
+        for o in (mB2, mB):
             mm(o, rot(0), rB1, False, False)
         for lo, hi in pieces:
             vgtt(("m" + u, lo, hi), full(win), ("LL", 48 + lo // 16, 48 + hi // 16), ("t" + u, lo, hi), A.add)
         sgat(rB2, full(win), ("LL", 72, 96))
-        for o in (mB, mB2):
+        for o in (mB2, mB):
             mm(o, rot(0), rB2, False, True)
         if t == 2:
             check(t, mA, mB, mB2, "W2", me * S4)
@@ -352,10 +353,13 @@ def rank_program(g, core, T, topo):
         turn("VW", 0, [q * me for q in range(N)], ["b0", "b1"], "vs", {me: blk("R3", me)})
     else:
         vcopy(blk("VW", 0), blk("R3", 0))
-    vgtt(("yt", 0, V), full("VW"), ("vl16", 0, 16), full("xb"), A.add)
+    ends = ((0, 128), (128, 256))
     sgat(("yt", 2 * V, 3 * V), full("VW"), ("vl16", 32, 48))
-    vgtt(("yt", V, 2 * V), full("VW"), ("vl16", 16, 32), ("yt", 0, V), A.add)
-    for lo, hi in ((0, 128), (128, 256)):
+    for lo, hi in ends:
+        vgtt(("yt", lo, hi), full("VW"), ("vl16", lo // 16, hi // 16), ("xb", lo, hi), A.add)
+    for lo, hi in ends:
+        vgtt(("yt", V + lo, V + hi), full("VW"), ("vl16", 16 + lo // 16, 16 + hi // 16), ("yt", lo, hi), A.add)
+    for lo, hi in ends:
         vtt(("yo", lo, hi), ("yt", V + lo, V + hi), ("yt", 2 * V + lo, 2 * V + hi), A.add)
     op("y", lambda: g.sync.dma_start(T.y[:, 0:128], T.yo[:, 0:128]), [("yo", 0, 128)], [], "dy0")
     op("s", lambda: sca.dma_start(T.y[:, 128:256], T.yo[:, 128:256]), [("yo", 128, 256)], [], "dy1")

@@ -11,30 +11,32 @@ SCRATCH = {
     "xb": ("sbuf", [128, V], "bfloat16"),
     "sn16": ("sbuf", [128, 56], "uint16"), "pl16": ("sbuf", [128, 48], "uint16"), "vl16": ("sbuf", [128, 48], "uint16"),
     "ones": ("sbuf", [128, 256], "bfloat16"), "E2": ("sbuf", [128, 256], "bfloat16"), "E2f": ("sbuf", [128, 256], "float32"),
-    "BO": ("sbuf", [128, 128], "bfloat16"), "BO2": ("sbuf", [128, 128], "bfloat16"), "BOf": ("sbuf", [128, 128], "float32"),
-    "I2": ("sbuf", [128, 128], "bfloat16"), "sz": ("sbuf", [128, 48], "bfloat16"),
-    "kkI": ("sbuf", [128, 48], "int32"), "kk16": ("sbuf", [128, 48], "uint16"),
-    "dg": ("sbuf", [128, 16], "int32"), "dg2": ("sbuf", [128, 16], "int32"),
-    "mask": ("sbuf", [128, E], "bfloat16"), "seg": ("sbuf", [128, E], "bfloat16"),
+    "I2": ("sbuf", [128, 128], "bfloat16"),
+    "Z": ("sbuf", [128, 3, 32], "int32"), "Z2": ("sbuf", [128, 96], "int32"), "Lw": ("sbuf", [128, 48], "int32"),
+    "Lp": ("sbuf", [128, 48], "uint16"),
+    "p1": ("sbuf", [128, 48], "int32"), "p2": ("sbuf", [128, 48], "int32"), "p3": ("sbuf", [128, 48], "int32"),
+    "p4": ("sbuf", [128, 48], "int32"), "plp": ("sbuf", [128, 48], "uint16"),
     "XS": ("sbuf", [128, S4], "bfloat16"), "XW": ("sbuf", [128, S4], "bfloat16"), "xe": ("sbuf", [128, E], "bfloat16"),
-    "vt": ("sbuf", [128, 48], "float32"), "Qw": ("sbuf", [128, 48], "float32"), "QB": ("sbuf", [128, E], "float32"),
-    "QF": ("sbuf", [128, E], "float32"), "QS": ("sbuf", [128, S4], "float32"), "QW": ("sbuf", [128, S4], "float32"),
-    "QG": ("sbuf", [128, E], "float32"), "QC": ("sbuf", [128, E], "float32"), "qi": ("sbuf", [128, 48], "int32"),
-    "ee": ("sbuf", [128, 96], "int32"), "LL": ("sbuf", [128, 96], "uint16"), "vi": ("sbuf", [128, 48], "int32"),
-    "vq": ("sbuf", [128, 48], "float32"), "vq2": ("sbuf", [128, 48], "float32"), "vp": ("sbuf", [128, 48], "float32"),
-    "W1": ("sbuf", [128, N * S4], "bfloat16"), "W2": ("sbuf", [128, N * S4], "bfloat16"),
-    "R3": ("sbuf", [128, S4], "bfloat16"), "VW": ("sbuf", [128, S4], "bfloat16"),
+    "w0": ("sbuf", [128, CAP], "float32"), "wq": ("sbuf", [128, S4], "float32"),
+    "GH": ("sbuf", [128, E], "float32"), "GL": ("sbuf", [128, E], "float32"),
+    "QS": ("sbuf", [128, S4], "float32"), "QW": ("sbuf", [128, S4], "float32"), "QG": ("sbuf", [128, E], "float32"),
+    "qf": ("sbuf", [128, 48], "float32"), "qi": ("sbuf", [128, 48], "int32"),
+    "ee": ("sbuf", [128, 96], "int32"), "LL": ("sbuf", [128, 96], "uint16"),
+    "jj": ("sbuf", [128, E], "int32"), "INV": ("sbuf", [128, S4], "int32"), "ivI": ("sbuf", [128, 56], "int32"),
+    "iv": ("sbuf", [128, 56], "uint16"),
+    "W1": ("sbuf", [128, N * S4], "bfloat16"), "W2": ("sbuf", [128, N * S4], "bfloat16"), "Rd": ("sbuf", [128, E], "bfloat16"),
+    "R3": ("sbuf", [128, S4], "bfloat16"), "VW": ("sbuf", [128, S4], "bfloat16"), "mg": ("sbuf", [128, E], "bfloat16"),
     "yt": ("sbuf", [128, E], "bfloat16"), "yo": ("sbuf", [128, V], "float32"),
 }
 for _t in "123":
-    for _n, _w in (("t", H), ("m", H), ("r", E), ("n", E), ("aA", H), ("aB", H), ("L", 256), ("z", E), ("mg", E)):
+    for _n, _w in (("t", H), ("m", H), ("r", E), ("n", E), ("aA", H), ("aB", H), ("L", 256), ("z", E)):
         SCRATCH[_n + _t] = ("sbuf", [128, _w], "bfloat16")
     for _n in ("f1", "f2", "f3"):
         SCRATCH[_n + "_" + _t] = ("sbuf", [128, M], "bfloat16")
 BANKS = ["b%d" % i for i in range(8)]
 for _b in BANKS:
     SCRATCH[_b] = ("psum", [128, 512], "float32")
-SEMAPHORES = ["cv", "cs", "cp", "cg", "dsn", "dx", "dpl", "dvl", "dy0", "dy1", "lx", "lq", "l1", "l2", "l3"]
+SEMAPHORES = ["cv", "cs", "cp", "cg", "dsn", "dx", "dpl", "dvl", "dz", "div", "dq", "dy0", "dy1", "lx", "lq", "l1", "l2", "l3"]
 SEMAPHORES += ["%s%d" % (k, p) for k in ("ax", "aq", "a1_", "a2_", "a3_") for p in range(N)]
 COMPUTE = {"v": "cv", "s": "cs", "p": "cp", "g": "cg"}
 
@@ -104,7 +106,8 @@ def rank_program(g, core, T, topo):
         return
     op, arrive, finish = tracker(g, T)
     vec, sca, ten = g.vector, g.scalar, g.tensor
-    others = sorted([r for r in range(N) if r != me], key=lambda r: (topo.die(T.cores[r]) != topo.die(core), (r - me) % N))
+    far = [topo.die(T.cores[r]) != topo.die(core) for r in range(N)]
+    others = sorted([r for r in range(N) if r != me], key=lambda r: (far[r], (r + me) % N))
 
     def ap(r):
         return T[r[0]][:, r[1]:r[2]]
@@ -114,6 +117,9 @@ def rank_program(g, core, T, topo):
 
     def blk(name, k):
         return (name, k * CAP, k * CAP + CAP)
+
+    def at(name, p, o=0):
+        return (name, o + p[0], o + p[1])
 
     def ind(r, l):
         return ap(r).indirect(ap(l))
@@ -128,8 +134,9 @@ def rank_program(g, core, T, topo):
     def vtt(o, a, b, f): op("v", lambda: vec.tensor_tensor(ap(o), ap(a), ap(b), f), [a, b], [o])
     def vgat(o, w, l): op("v", lambda: vec.tensor_copy(ap(o), ind(w, l)), [w, l], [o])
     def vgtt(o, w, l, b, f): op("v", lambda: vec.tensor_tensor(ap(o), ind(w, l), ap(b), f), [w, l, b], [o])
+    def vsca(o, l, a, b, f): op("v", lambda: vec.tensor_tensor(ind(o, l), ap(a), ap(b), f), [a, b, l], [o])
     def act(o, i, f=F.Copy, **k): op("s", lambda: sca.activation(ap(o), ap(i), f, **k), [i], [o])
-    def sgat(o, w, l): op("s", lambda: sca.activation(ap(o), ind(w, l), F.Copy), [w, l], [o])
+    def sgat(o, w, l, **k): op("s", lambda: sca.activation(ap(o), ind(w, l), F.Copy, **k), [w, l], [o])
     def mm(o, w, i, start=True, stop=True): op("p", lambda: ten.matmul(ap(o), ap(w), ap(i), start, stop), [w, i], [o])
 
     def rot(k, name="E2"):
@@ -144,38 +151,34 @@ def rank_program(g, core, T, topo):
         return RemoteDMATransfer(srcs=[ap(s) for s in srcs], dsts=[ap(d) for d in dsts], dst_ids=ids,
                                  dma_engine_mask=sum(1 << e for e in engines), remote_sem=T.sem[sem_arr])
 
-    def send(pairs, sem_arr, sem_loc):
-        tr, n = [], 0
-        for i, (r, s, d) in enumerate(pairs):
+    def send(src, dst, key, sem_loc):
+        tr, k = [], 0
+        for r in others:
             e = topo.engines(core, T.cores[r])
             n = len(e) // 4
-            tr.append(transfer([s], [d], [r], e[n * i:n * i + n], sem_arr))
+            if far[r]:
+                e = e[0::2][n * k:n * k + n]
+                k += 1
+            else:
+                e = e[1::2][:n]
+            tr.append(transfer([blk(src, r)], [blk(dst, me)], [r], e, "%s%d" % (key, me)))
 
         def call():
             g.remote_dma_fused(tr, local_sem=T.sem[sem_loc])
-        op("g", call, [s for _, s, _ in pairs], [], sem_loc, len(pairs) * n)
-        return n
+        op("g", call, [blk(src, r) for r in others], [], sem_loc, len(others) * n)
+        for r in others:
+            arrive("%s%d" % (key, r), n, blk(dst, r))
 
-    def send_all(src, sem_arr, sem_loc):
+    def send_all(win, key, sem_loc):
+        src = (win, me * S4, me * S4 + S4)
         e = topo.engines(core, T.cores[others[0]])
-        tr = transfer([src], [src] * len(others), others, e, sem_arr)
+        tr = transfer([src], [src] * len(others), others, e, "%s%d" % (key, me))
 
         def call():
             g.remote_dma_fused([tr], local_sem=T.sem[sem_loc])
         op("g", call, [src], [], sem_loc, len(e))
-        return len(e)
-
-    def widen(name, copy):
-        w, steps = 16, []
-        while w < E:
-            n = min(w, E - w)
-            steps.append(lambda w=w, n=n: copy((name, w, w + n), (name, 0, n)))
-            w += n
-        return steps
-
-    def zeros(name, base):
-        for k in range(N):
-            act((name, base + k * CAP, base + k * CAP + CAP), ("ones", 0, CAP), F.Copy, scale=0.0)
+        for r in others:
+            arrive("%s%d" % (key, r), len(e), (win, r * S4, r * S4 + S4))
 
     own = (me * S4, me * S4 + S4)
     op("y", lambda: g.sync.dma_start(T.snI[:], T.sn[:]), [], [full("snI")], "dsn")
@@ -183,20 +186,20 @@ def rank_program(g, core, T, topo):
     op("y", lambda: g.sync.dma_start(T.vlI[:], T.vl[:]), [], [full("vlI")], "dvl")
     op("s", lambda: sca.dma_start(T.plI[:], T.pl[:]), [], [full("plI")], "dpl")
     vset(full("ones"), 1.0)
-    op("g", lambda: g.iota(T.dg[:], [[-1, 16]], 112, 1), [], [full("dg")])
-    op("g", lambda: g.iota(T.kkI[:], [[1, 48]], 0, 0), [], [full("kkI")])
+    ZZ = ("Z", 0, 96)
+    op("v", lambda: vec.memset(T.Z[:], 0), [], [ZZ])
+    for h in range(8):
+        def call(r=16 * h, c=16 * (h % 2)):
+            return g.sync.dma_start(T.Z[r:r + 16, :, c:c + 16], T.pl[r:r + 16, :])
+        op("y", call, [], [("Z", 96 + h, 97 + h)] if h else [ZZ, ("Z", 96, 97)], "dz")
+    op("g", lambda: g.iota(T.w0[:], [[1, CAP]], me * CAP, 0, allow_small_or_imprecise_dtypes=True), [], [full("w0")])
     op("g", lambda: g.affine_select(T.E2[:], T.ones[:], [[0, 2], [-1, 128]], A.is_equal, 0.0, 0, 1), [full("ones")], [full("E2")])
-    op("g", lambda: g.affine_select(T.BO[:], T.ones[:, 0:128], [[-16, 8], [0, 16]], A.is_ge, 0.0, 0, 1), [("ones", 0, 128)], [full("BO")])
-    op("g", lambda: g.affine_select(T.BO2[:], T.BO[:], [[16, 8], [0, 16]], A.is_ge, 0.0, 15, -1), [full("BO")], [full("BO2")])
-    vts(full("dg2"), full("dg"), 15, A.bitwise_and)
-    vcopy(full("kk16"), full("kkI"))
-    vts(("mask", 0, 16), full("dg2"), 0, A.is_equal)
-    vset(full("sz"), 0.0)
-    vset(("W1",) + own, 0.0)
-    zeros("QS", 0)
-    mask = widen("mask", vcopy)
-    mask[0]()
-    mask[1]()
+    for k in range(N):
+        act(blk("QS", k), ("ones", 0, CAP), F.Copy, scale=0.0)
+    for q in range(N):
+        vts(blk("wq", q), full("w0"), float(q * S4), A.add)
+    act(full("E2f"), full("E2"))
+    act(full("I2"), ("E2", 0, 128), F.Copy, scale=2.0)
 
     vcopy(full("sn16"), full("snI"))
     def snl(q, lo=0, hi=14): return ("sn16", 14 * q + lo, 14 * q + hi)
@@ -205,162 +208,179 @@ def rank_program(g, core, T, topo):
     sgat(blk("XS", q1), full("xb"), snl(q1))
     vgat(("XS", q2 * CAP, q2 * CAP + 96), full("xb"), snl(q2, 0, 6))
     sgat(("XS", q2 * CAP + 96, q2 * CAP + CAP), full("xb"), snl(q2, 6, 14))
-    n = send([(q, blk("XS", q), blk("XW", me)) for q in others], "ax%d" % me, "lx")
-    for p in others:
-        arrive("ax%d" % p, n, blk("XW", p))
-    act(full("BOf"), full("BO2"))
-    sgat(blk("XW", me), full("xb"), snl(me))
-    act(full("E2f"), full("E2"))
-    act(full("I2"), ("E2", 0, 128), F.Copy, scale=2.0)
-
-    vts(full("vq"), full("vlI"), 111.5, A.subtract, 1.0 / CAP, A.mult)
-    mask[2]()
-    vcopy(full("vi"), full("vq"))
-    mask[3]()
-    vts(full("vq2"), full("vi"), float(S4 - CAP), A.mult)
     vcopy(full("vl16"), full("vlI"))
-    vtt(full("vp"), full("vlI"), full("vq2"), A.add)
-    mask[4]()
-    vts(full("vt"), full("vp"), 4096.0, A.mult, 4097.0 * CAP * me, A.add)
-    mask[5]()
-    for d in range(3):
-        a, b = (d + 1) % 3, (d + 2) % 3
-        vtt(("Qw", 16 * d, 16 * d + 16), ("vt", 16 * a, 16 * a + 16), ("vp", 16 * b, 16 * b + 16), A.add)
-    for d in range(3):
-        dd = (V * d, V * d + V)
-        vgtt(("QB",) + dd, full("Qw"), ("kk16", 16 * d, 16 * d + 16), ("mask",) + dd, A.mult)
-        mm(("b%d" % (5 + d), 0, V), full("BOf"), ("QB",) + dd)
-        act(("QF",) + dd, ("b%d" % (5 + d), 0, V))
-    vset(full("seg"), 1.0)
-    for d in range(3):
-        i, o, l = ("QF", V * d, V * d + V), full("QS"), ("vl16", 16 * d, 16 * d + 16)
-        op("v", lambda: vec.tensor_copy(ind(o, l), ap(i)), [i, l], [o])
-        if d == 0:
-            vcopy(full("pl16"), full("plI"))
-        elif d == 1:
-            op("v", lambda: vec.tensor_copy(T.seg[:, 0:E:16], T.sz[:]), [full("sz")], [full("seg")])
-    n = send([(q, blk("QS", q), blk("QW", me)) for q in others], "aq%d" % me, "lq")
-    for p in others:
-        arrive("aq%d" % p, n, blk("QW", p))
+    send("XS", "XW", "ax", "lx")
+    op("g", lambda: g.iota(T.INV[:], [[0, S4]], 0, 0), [], [full("INV")])
 
-    def turn(win, base, ks, banks, evac, src={}, ident="E2"):
-        for grp, bank, q in zip([[1, 2], [3]], banks, evac):
-            for i, p in enumerate(grp):
-                s = src.get(p, (win, base + p * CAP, base + p * CAP + CAP))
-                mm((bank, i * CAP, i * CAP + CAP), rot(ks[p], ident), s)
-            o = (win, base + grp[0] * CAP, base + grp[-1] * CAP + CAP)
-            i = (bank, 0, CAP * len(grp))
+    def vll(d): return ("vl16", 16 * d, 16 * d + 16)
+    def sec(n, d): return (n, V * d, V * d + V)
+    for d in range(3):
+        sgat(sec("GH", (d + 1) % 3), full("wq"), vll((d + 1) % 3), scale=4096.0)
+        sgat(sec("GL", (d + 2) % 3), full("wq"), vll((d + 2) % 3))
+    vgat(blk("XW", me), full("xb"), snl(me))
+    vcopy(full("pl16"), full("plI"))
+    vts(full("p1"), full("plI"), 4, A.logical_shift_right)
+    vts(full("p3"), full("plI"), 56.0, A.mult)
+    vts(full("p2"), full("p1"), -895.0, A.mult)
+    for b in range(3):
+        op("v", lambda: vec.transpose(T.Z2[:, 32 * b:32 * b + 32], T.Z[:, b, :]), [("Z", 0, 104)], [("Z2", 32 * b, 32 * b + 32)])
+    vtt(full("p4"), full("p3"), full("p2"), A.add)
+    for d in range(3):
+        vsca(full("QS"), vll(d), sec("GH", (d + 1) % 3), sec("GL", (d + 2) % 3), A.add)
+        op("v", lambda: vec.tensor_tensor(T.Lw[:, d:48:3], T.Z2[:, 32 * d:32 * d + 16], T.Z2[:, 32 * d + 16:32 * d + 32], A.add),
+           [("Z2", 32 * d, 32 * d + 32)], [("Lw", d, d + 1)])
+        if d == 0:
+            vcopy(full("plp"), full("p4"))
+    send("QS", "QW", "aq", "lq")
+    op("g", lambda: g.iota(T.W1[:, own[0]:own[1]], [[0, S4]], 0, 0, allow_small_or_imprecise_dtypes=True), [], [("W1",) + own])
+    op("g", lambda: g.iota(T.jj[:], [[1, E]], 0, 0), [], [full("jj")])
+    vcopy(full("Lp"), full("Lw"))
+
+    def turn(win, base, ks, plan, ident="E2", mine=None):
+        for p, bank, q in plan:
+            o = (win, base + p * CAP, base + p * CAP + CAP)
+            mm((bank, 0, CAP), rot(ks[p], ident), mine if mine and p == me else o)
             if q == "v":
-                vcopy(o, i)
+                vcopy(o, (bank, 0, CAP))
             else:
-                act(o, i)
+                act(o, (bank, 0, CAP))
+
+    def plan(banks, queues):
+        return list(zip([p for p in [me] + others if p], banks, queues))
 
     if me:
-        turn("XW", 0, [-p * me for p in range(N)], ["b0", "b1"], "sv")
+        turn("XW", 0, [-p * me for p in range(N)], plan(["b0", "b1", "b2"], "sss"))
+        mm(("b6", 0, CAP), rot(-me * me, "E2f"), blk("QS", me))
 
-    pieces = ((0, H // 2), (H // 2, H))
-    def plh(h): return ("pl16", 24 * h, 24 * h + 24)
-    def check(t, mA, mB, mB2, out, base):
-        u = str(t)
-        aA, aB, pB = full("aA" + u), full("aB" + u), ("b1", 0, H)
-        act(aA, mA, F.Abs, scale=4.0)
-        act(pB, mB, F.Abs, scale=4.0)
-        for lo, hi in pieces:
-            vts(("n" + u, lo, hi), (mA[0], lo, hi), 0.0, A.is_ge, 0.5, A.subtract)
-        vts(("n" + u, H, E), mB2, 0.0, A.is_ge, 0.5, A.subtract)
-        if t > 1:
-            vts(aA, aA, 4.0 * B, A.min)
-        for e in range(6):
+    P0, P1, PH = (0, 256), (256, H), (0, H)
+    def sign(u, src, p, o=0): vts(at("n" + u, p, o), src, 0.0, A.is_ge, 0.5, A.subtract)
+    def total(u, es):
+        for e in es:
             mm(("b4", 0, M), full("I2"), ("n" + u, e * M, e * M + M), e == 0, e == 5)
-        act(aB, mB, F.Abs, scale=4.0)
+    def fold(u):
+        act(full("f1_" + u), ("b4", 0, M), F.Abs)
+        act(full("f2_" + u), full("f1_" + u), F.Abs, bias=-4.0)
+    def parity(u):
+        vts(full("f3_" + u), full("f2_" + u), 2.0, A.is_equal, 0.5, A.subtract)
+        for i in range(3):
+            mm(("b5", i * M, i * M + M), rot(0), full("f3_" + u))
+    def plc(lo, hi): return ("pl16", lo // 16, hi // 16)
+
+    u = "1"
+    sgat(("xe", H, 640), full("XW"), plc(H, 640))
+    vgat(("xe", 0, H), full("XW"), plc(0, H))
+    sign(u, at("xe", PH), PH)
+    vgat(("xe", 640, E), full("XW"), plc(640, E))
+    act(at("b1", P0), at("xe", P0, H), F.Abs, scale=4.0)
+    act(at("aA1", P0), at("xe", P0), F.Abs, scale=4.0)
+    sign(u, at("xe", PH, H), PH, H)
+    total(u, range(6))
+    act(at("b2", P1), at("xe", P1, H), F.Abs, scale=4.0)
+    act(at("aA1", P1), at("xe", P1), F.Abs, scale=4.0)
+    L0, L1, L01, L2 = ("L1", 0, 128), ("L1", 128, 256), ("L1", 0, 256), ("b3", H, 512)
+    vtt(L01, at("aA1", P0), at("b1", P0), A.min)
+    fold(u)
+    act(full("aB1"), at("xe", PH, H), F.Abs, scale=4.0)
+    vtt(L2, at("aA1", P1), at("b2", P1), A.min)
+    vtt(("b3", 256, 384), L0, L1, A.min)
+    vtt(("b3", 0, 128), L1, L2, A.min)
+    vtt(("b3", 128, 256), L0, L2, A.min)
+    vtt(at("mg", P1, H), at("aA1", P1), at("b3", P1), A.min)
+    parity(u)
+    vtt(at("mg", P0, H), at("aA1", P0), at("b3", P0), A.min)
+    vtt(at("mg", PH), full("aB1"), at("b3", PH), A.min)
+    for o in (0, H):
+        vtt(at("z1", PH, o), at("n1", PH, o), at("b5", PH), A.mult)
+    vsca(("W1",) + own, full("pl16"), full("z1"), full("mg"), A.mult)
+    send_all("W1", "a1_", "l1")
+
+    if me:
+        act(blk("QW", me), ("b6", 0, CAP))
+        turn("QW", 0, [-p * me for p in range(N)], plan(["b6", "b7", "b0"], "sss")[1:], "E2f")
+    else:
+        act(blk("QW", 0), blk("QS", 0))
+    sgat(full("QG"), full("QW"), full("Lp"))
+    op("y", lambda: g.sync.dma_start(T.qf[:], T.QG[0:128:16, :]), [full("QG")], [full("qf")], "dq")
+    op("v", lambda: vec.tensor_copy(ind(full("INV"), full("plp")), ap(full("jj"))), [full("jj"), full("plp")], [full("INV")])
+    op("y", lambda: g.sync.dma_start(T.ivI[:], T.INV[0:128:16, :]), [full("INV")], [full("ivI")], "div")
+
+    for t, win, out, base in ((2, "W1", "W2", me * S4), (3, "W2", "R3", 0)):
+        u = str(t)
+        for i, q in enumerate(others):
+            if t == 2 and i == 2:
+                vcopy(full("qi"), full("qf"))
+                vts(("ee", 0, 48), full("qi"), 12, A.logical_shift_right)
+                vts(("ee", 48, 96), full("qi"), 4095, A.bitwise_and)
+                vcopy(full("LL"), full("ee"))
+            banks = ["b%d" % (3 * (i % 2) + j) for j in range(3)]
+            turn(win, q * S4, [-p * (me - q) for p in range(N)], list(zip((1, 2, 3), banks, "vsv")))
+        aA, aB, rA = "aA" + u, "aB" + u, "r" + u
+        mb = {P0: at("b7", P0), P1: at("b6", P1)}
+        for p in (P0, P1):
+            mm(mb[p], rot(0), at("xe", p, H), True, False)
+        sgat(at(rA, PH), full(win), ("LL", 24, 48))
+        for p in (P0, P1):
+            vgtt(at("t" + u, p), full(win), ("LL", p[0] // 16, p[1] // 16), at("xe", p), A.add)
+            mm(mb[p], rot(0), at(rA, p), False, False)
+        sgat(at(rA, P0, H), full(win), ("LL", 72, 88))
+        mm(mb[P0], rot(0), at(rA, P0, H), False, True)
+        vgtt(at("m" + u, P0), full(win), ("LL", 48, 64), at("t" + u, P0), A.add)
+        vgat(at(rA, P1, H), full(win), ("LL", 88, 96))
+        mm(mb[P1], rot(0), at(rA, P1, H), False, True)
+        vgtt(at("m" + u, P1), full(win), ("LL", 64, 72), at("t" + u, P1), A.add)
+        act(at(aA, P0), at("m" + u, P0), F.Abs, scale=4.0)
+        if t == 2:
+            vcopy(full("iv"), full("ivI"))
+        for p in (P0, P1):
+            sign(u, at("m" + u, p), p)
+        total(u, range(3))
+        act(at("b1", P0), mb[P0], F.Abs, scale=4.0)
+        act(at(aA, P1), at("m" + u, P1), F.Abs, scale=4.0)
+        act(at("b2", P1), mb[P1], F.Abs, scale=4.0)
+        vts(at(aA, P0), at(aA, P0), 4.0 * B, A.min)
         L0, L1, L01, L2 = ("L" + u, 0, 128), ("L" + u, 128, 256), ("L" + u, 0, 256), ("b3", H, 512)
-        vtt(L01, ("aA" + u, 0, 256), ("b1", 0, 256), A.min)
-        vtt(L2, ("aA" + u, 256, H), ("b1", 256, H), A.min)
-        f1, f2, f3 = full("f1_" + u), full("f2_" + u), full("f3_" + u)
-        act(f1, ("b4", 0, M), F.Abs)
+        vtt(L01, at(aA, P0), at("b1", P0), A.min)
+        sign(u, mb[P0], P0, H)
+        vtt(L2, at(aA, P1), at("b2", P1), A.min)
+        sign(u, mb[P1], P1, H)
+        total(u, range(3, 6))
+        for p in (P0, P1):
+            act(at(aB, p), mb[p], F.Abs, scale=4.0)
         vtt(("b3", 256, 384), L0, L1, A.min)
         vtt(("b3", 0, 128), L1, L2, A.min)
         vtt(("b3", 128, 256), L0, L2, A.min)
-        act(f2, f1, F.Abs, bias=-4.0)
-        vts(f3, f2, 2.0, A.is_equal, 0.5, A.subtract)
-        for i in range(3):
-            mm(("b5", i * M, i * M + M), rot(0), f3)
-        for lo, hi in ((256, H), (0, 256)):
-            vtt(("mg" + u, H + lo, H + hi), ("aA" + u, lo, hi), ("b3", lo, hi), A.min)
-        vtt(("mg" + u, 0, H), aB, ("b3", 0, H), A.min)
-        for lo, hi in ((0, H), (H, E)):
-            vtt(("z" + u, lo, hi), ("n" + u, lo, hi), ("b5", 0, H), A.mult)
-        o, l = (out, base, base + S4), full("pl16")
-        op("v", lambda: vec.tensor_tensor(ind(o, l), ap(full("z" + u)), ap(full("mg" + u)), A.mult),
-           [full("z" + u), full("mg" + u), l], [o])
-
-    vgat(("xe", 0, H), full("XW"), plh(0))
-    sgat(("xe", H, E), full("XW"), plh(1))
-    check(1, ("xe", 0, H), ("xe", H, E), ("xe", H, E), "W1", me * S4)
-    n = send_all(("W1",) + own, "a1_%d" % me, "l1")
-    for q in others:
-        arrive("a1_%d" % q, n, ("W1", q * S4, q * S4 + S4))
-
-    if me:
-        turn("QW", 0, [-p * me for p in range(N)], ["b6", "b7"], "ss", {me: blk("QS", me)}, "E2f")
-    else:
-        act(blk("QW", 0), blk("QS", 0))
-    zeros("W2", me * S4)
-    hs = [(H * h, H * h + H) for h in range(2)]
-    for h in range(2):
-        vgtt(("QG",) + hs[h], full("QW"), plh(h), ("mask",) + hs[h], A.mult)
-    for lo, hi in hs:
-        op("v", lambda: vec.tensor_tensor_scan(T.QC[:, lo:hi], T.seg[:, lo:hi], T.QG[:, lo:hi], 0.0, A.mult, A.add),
-           [("seg", lo, hi), ("QG", lo, hi)], [("QC", lo, hi)])
-    for lo, hi in hs:
-        op("v", lambda: vec.tensor_copy(T.qi[:, lo // 16:hi // 16], T.QC[:, lo + 15:hi:16]), [("QC", lo, hi)], [("qi", lo // 16, hi // 16)])
-    for c, k, f in ((0, 12, A.logical_shift_right), (48, 4095, A.bitwise_and)):
-        for h in range(2):
-            vts(("ee", c + 24 * h, c + 24 * h + 24), ("qi", 24 * h, 24 * h + 24), k, f)
-    for c in (0, 48):
-        vcopy(("LL", c, c + 48), ("ee", c, c + 48))
-
-    for t, win in ((2, "W1"), (3, "W2")):
-        u = str(t)
-        for i, (q, ev) in enumerate(zip(others, ("vs", "vs", "sv"))):
-            turn(win, q * S4, [-p * (me - q) for p in range(N)], ["b%d" % (2 * i), "b%d" % (2 * i + 1)], ev)
-        mA, rB1, rB2, mB, mB2 = full("m" + u), ("r" + u, 0, H), ("r" + u, H, E), ("b7", 0, H), ("b6", 0, H)
-        for o in (mB2, mB):
-            mm(o, rot(0), ("xe", H, E), True, False)
-        for lo, hi in pieces:
-            vgtt(("t" + u, lo, hi), full(win), ("LL", lo // 16, hi // 16), ("xe", lo, hi), A.add)
-        sgat(rB1, full(win), ("LL", 24, 48))
-        for o in (mB2, mB):
-            mm(o, rot(0), rB1, False, False)
-        for lo, hi in pieces:
-            vgtt(("m" + u, lo, hi), full(win), ("LL", 48 + lo // 16, 48 + hi // 16), ("t" + u, lo, hi), A.add)
-        sgat(rB2, full(win), ("LL", 72, 96))
-        for o in (mB2, mB):
-            mm(o, rot(0), rB2, False, True)
+        fold(u)
+        vtt(at("b2", P1), at(aA, P1), at("b3", P1), A.min)
+        vtt(at("b2", P0), at(aA, P0), at("b3", P0), A.min)
+        vtt(at("b0", PH), full(aB), at("b3", PH), A.min)
+        parity(u)
+        vtt(at("z" + u, PH, H), at("n" + u, PH, H), at("b2", PH), A.mult)
+        vtt(at("z" + u, PH), at("n" + u, PH), at("b0", PH), A.mult)
+        for o in (H, 0):
+            vtt(at("Rd", PH, o), at("z" + u, PH, o), at("b5", PH), A.mult)
+        k = 30
+        sgat((out, base + 16 * k, base + S4), full("Rd"), ("iv", k, 56))
+        vgat((out, base, base + 16 * k), full("Rd"), ("iv", 0, k))
         if t == 2:
-            check(t, mA, mB, mB2, "W2", me * S4)
-            n = send_all(("W2",) + own, "a2_%d" % me, "l2")
-            for q in others:
-                arrive("a2_%d" % q, n, ("W2", q * S4, q * S4 + S4))
-            zeros("R3", 0)
+            send_all("W2", "a2_", "l2")
         else:
-            check(t, mA, mB, mB2, "R3", 0)
-            n = send([(p, blk("R3", p), blk("VW", me)) for p in others], "a3_%d" % me, "l3")
-            for q in others:
-                arrive("a3_%d" % q, n, blk("VW", q))
+            send("R3", "VW", "a3_", "l3")
 
     if me:
-        turn("VW", 0, [q * me for q in range(N)], ["b0", "b1"], "vs", {me: blk("R3", me)})
+        turn("VW", 0, [q * me for q in range(N)], plan(["b0", "b1", "b2"], "svs"), mine=blk("R3", me))
     else:
         vcopy(blk("VW", 0), blk("R3", 0))
-    ends = ((0, 128), (128, 256))
-    sgat(("yt", 2 * V, 3 * V), full("VW"), ("vl16", 32, 48))
-    for lo, hi in ends:
-        vgtt(("yt", lo, hi), full("VW"), ("vl16", lo // 16, hi // 16), ("xb", lo, hi), A.add)
-    for lo, hi in ends:
-        vgtt(("yt", V + lo, V + hi), full("VW"), ("vl16", 16 + lo // 16, 16 + hi // 16), ("yt", lo, hi), A.add)
-    for lo, hi in ends:
-        vtt(("yo", lo, hi), ("yt", V + lo, V + hi), ("yt", 2 * V + lo, 2 * V + hi), A.add)
+    P, Q = (0, 128), (128, 256)
+    sgat(at("yt", P, 2 * V), full("VW"), ("vl16", 32, 40))
+    vgtt(at("yt", P), full("VW"), ("vl16", 0, 8), at("xb", P), A.add)
+    vgtt(at("yt", Q), full("VW"), ("vl16", 8, 16), at("xb", Q), A.add)
+    sgat(at("yt", Q, V), full("VW"), ("vl16", 24, 32))
+    vgtt(at("yt", P, V), full("VW"), ("vl16", 16, 24), at("yt", P), A.add)
+    mm(("b3", 0, 128), rot(0), at("yt", Q, V), True, False)
+    sgat(at("yt", Q, 2 * V), full("VW"), ("vl16", 40, 48))
+    mm(("b3", 0, 128), rot(0), at("yt", Q, 2 * V), False, True)
+    vtt(at("yo", P), at("yt", P, V), at("yt", P, 2 * V), A.add)
+    vtt(at("yo", Q), at("yt", Q), ("b3", 0, 128), A.add)
     op("y", lambda: g.sync.dma_start(T.y[:, 0:128], T.yo[:, 0:128]), [("yo", 0, 128)], [], "dy0")
     op("s", lambda: sca.dma_start(T.y[:, 128:256], T.yo[:, 128:256]), [("yo", 128, 256)], [], "dy1")
     finish()

import numpy as np
from concourse.bass import DstId, RemoteDMATransfer
from concourse.mybir import AluOpType as A, ActivationFunctionType as F

N, V, M, CAP, B = 4, 256, 128, 224, 63
E = 768
S4 = N * CAP
H = E // 2
SCRATCH = {
    "snI": ("sbuf", [128, 56], "int32"), "plI": ("sbuf", [128, 48], "int32"), "vlI": ("sbuf", [128, 48], "int32"),
    "xb": ("sbuf", [128, V], "bfloat16"),
    "sn16": ("sbuf", [128, 56], "uint16"), "pl16": ("sbuf", [128, 48], "uint16"), "vl16": ("sbuf", [128, 48], "uint16"),
    "ones": ("sbuf", [128, 256], "bfloat16"), "E2": ("sbuf", [128, 256], "bfloat16"), "E2f": ("sbuf", [128, 256], "float32"),
    "I2": ("sbuf", [128, 128], "bfloat16"),
    "Z": ("sbuf", [128, 3, 32], "int32"), "Z2": ("sbuf", [128, 96], "int32"), "Lw": ("sbuf", [128, 48], "int32"),
    "Lp": ("sbuf", [128, 48], "uint16"),
    "p1": ("sbuf", [128, 48], "int32"), "p2": ("sbuf", [128, 48], "int32"), "p3": ("sbuf", [128, 48], "int32"),
    "p4": ("sbuf", [128, 48], "int32"), "plp": ("sbuf", [128, 48], "uint16"),
    "XS": ("sbuf", [128, S4], "bfloat16"), "XW": ("sbuf", [128, S4], "bfloat16"), "xe": ("sbuf", [128, E], "bfloat16"),
    "w0": ("sbuf", [128, CAP], "float32"), "wq": ("sbuf", [128, S4], "float32"),
    "GH": ("sbuf", [128, E], "float32"), "GL": ("sbuf", [128, E], "float32"),
    "QS": ("sbuf", [128, S4], "float32"), "QW": ("sbuf", [128, S4], "float32"), "QG": ("sbuf", [128, E], "float32"),
    "qf": ("sbuf", [128, 48], "float32"), "qi": ("sbuf", [128, 48], "int32"),
    "ee": ("sbuf", [128, 96], "int32"), "LL": ("sbuf", [128, 96], "uint16"),
    "jj": ("sbuf", [128, E], "int32"), "INV": ("sbuf", [128, S4], "int32"), "ivI": ("sbuf", [128, 56], "int32"),
    "iv": ("sbuf", [128, 56], "uint16"),
    "W1": ("sbuf", [128, N * S4], "bfloat16"), "W2": ("sbuf", [128, N * S4], "bfloat16"), "Rd": ("sbuf", [128, E], "bfloat16"),
    "R3": ("sbuf", [128, S4], "bfloat16"), "VW": ("sbuf", [128, S4], "bfloat16"), "mg": ("sbuf", [128, E], "bfloat16"),
    "yt": ("sbuf", [128, E], "bfloat16"), "yo": ("sbuf", [128, V], "float32"),
}
for _t in "123":
    for _n, _w in (("t", H), ("m", H), ("r", E), ("n", E), ("aA", H), ("aB", H), ("L", 256), ("z", E)):
        SCRATCH[_n + _t] = ("sbuf", [128, _w], "bfloat16")
    for _n in ("f1", "f2", "f3"):
        SCRATCH[_n + "_" + _t] = ("sbuf", [128, M], "bfloat16")
BANKS = ["b%d" % i for i in range(8)]
for _b in BANKS:
    SCRATCH[_b] = ("psum", [128, 512], "float32")
SEMAPHORES = ["cv", "cs", "cp", "cg", "dsn", "dx", "dpl", "dvl", "dz", "div", "dq", "dy0", "dy1", "lx", "lq", "l1", "l2", "l3"]
SEMAPHORES += ["%s%d" % (k, p) for k in ("ax", "aq", "a1_", "a2_", "a3_") for p in range(N)]
COMPUTE = {"v": "cv", "s": "cs", "p": "cp", "g": "cg"}


def tracker(g, T):
    eng = {"v": g.vector, "s": g.scalar, "p": g.tensor, "g": g, "y": g.sync}
    acc, clk, done, cnt = {}, {q: {} for q in eng}, {}, {}

    def wait(q, req):
        for s in sorted(req):
            if any(o != s and done.get((o, req[o]), {}).get(s, 0) >= req[s] for o in req):
                continue
            if clk[q].get(s, 0) < req[s]:
                eng[q].wait_ge(T.sem[s], req[s])
        for s in req:
            for k, v in list(done.get((s, req[s]), {}).items()) + [(s, req[s])]:
                clk[q][k] = max(clk[q].get(k, 0), v)

    def needs(q, who, reads, writes):
        req = {}
        for lst, w in ((reads, False), (writes, True)):
            for b, lo, hi in lst:
                bank = b in BANKS
                for (l2, h2, w2, q2, s, v) in acc.get(b, []):
                    same = q2 == who
                    if bank and not same:
                        hit = True
                    else:
                        hit = (w or w2) and lo < h2 and l2 < hi
                        if same and (not w2 or (bank and who == "p")):
                            hit = False
                    if hit:
                        req[s] = max(req.get(s, 0), v)
        return req

    def note(who, reads, writes, s, v):
        for lst, w in ((reads, False), (writes, True)):
            for b, lo, hi in lst:
                acc.setdefault(b, []).append((lo, hi, w, who, s, v))

    def op(q, call, reads, writes, sem=None, inc=16):
        who = q if sem is None else "dma"
        wait(q, needs(q, who, reads, writes))
        if sem is None:
            sem, inc = COMPUTE[q], 1
        cnt[sem] = cnt.get(sem, 0) + inc
        r = call()
        if r is not None:
            r.then_inc(T.sem[sem], inc)
        note(who, reads, writes, sem, cnt[sem])
        c = dict(clk[q]); c[sem] = cnt[sem]
        if who != "dma":
            done[(sem, cnt[sem])] = c

    def arrive(sem, n, region):
        cnt[sem] = cnt.get(sem, 0) + n
        note("rx", [], [region], sem, cnt[sem])

    def finish():
        wait("g", dict(cnt))
    return op, arrive, finish


def rank_program(g, core, T, topo):
    me = T.rank_of(core)
    if me is None:
        return
    op, arrive, finish = tracker(g, T)
    vec, sca, ten = g.vector, g.scalar, g.tensor
    far = [topo.die(T.cores[r]) != topo.die(core) for r in range(N)]
    others = sorted([r for r in range(N) if r != me], key=lambda r: (far[r], (r + me) % N))

    def ap(r):
        return T[r[0]][:, r[1]:r[2]]

    def full(n):
        return (n, 0, SCRATCH[n][1][1])

    def blk(name, k):
        return (name, k * CAP, k * CAP + CAP)

    def at(name, p, o=0):
        return (name, o + p[0], o + p[1])

    def ind(r, l):
        return ap(r).indirect(ap(l))

    def vcopy(o, i): op("v", lambda: vec.tensor_copy(ap(o), ap(i)), [i], [o])
    def vset(o, c): op("v", lambda: vec.memset(ap(o), c), [], [o])
    def vts(o, i, s1, o1, s2=None, o2=None):
        if o2 is None:
            op("v", lambda: vec.tensor_scalar(ap(o), ap(i), s1, None, o1), [i], [o])
        else:
            op("v", lambda: vec.tensor_scalar(ap(o), ap(i), s1, s2, o1, o2), [i], [o])
    def vtt(o, a, b, f): op("v", lambda: vec.tensor_tensor(ap(o), ap(a), ap(b), f), [a, b], [o])
    def vgat(o, w, l): op("v", lambda: vec.tensor_copy(ap(o), ind(w, l)), [w, l], [o])
    def vgtt(o, w, l, b, f): op("v", lambda: vec.tensor_tensor(ap(o), ind(w, l), ap(b), f), [w, l, b], [o])
    def vsca(o, l, a, b, f): op("v", lambda: vec.tensor_tensor(ind(o, l), ap(a), ap(b), f), [a, b, l], [o])
    def act(o, i, f=F.Copy, **k): op("s", lambda: sca.activation(ap(o), ap(i), f, **k), [i], [o])
    def sgat(o, w, l, **k): op("s", lambda: sca.activation(ap(o), ind(w, l), F.Copy, **k), [w, l], [o])
    def mm(o, w, i, start=True, stop=True): op("p", lambda: ten.matmul(ap(o), ap(w), ap(i), start, stop), [w, i], [o])

    def rot(k, name="E2"):
        a = 16 * (k % 8)
        return (name, a, a + 128)

    def transfer(srcs, dsts, ranks, engines, sem_arr):
        ids = []
        for r in ranks:
            rid, pid = topo.addr(T.cores[r])[:2]
            ids.append(DstId(rid=rid, pnc=pid))
        return RemoteDMATransfer(srcs=[ap(s) for s in srcs], dsts=[ap(d) for d in dsts], dst_ids=ids,
                                 dma_engine_mask=sum(1 << e for e in engines), remote_sem=T.sem[sem_arr])

    def send(src, dst, key, sem_loc):
        tr, k = [], 0
        for r in others:
            e = topo.engines(core, T.cores[r])
            n = len(e) // 4
            if far[r]:
                e = e[0::2][n * k:n * k + n]
                k += 1
            else:
                e = e[1::2][:n]
            tr.append(transfer([blk(src, r)], [blk(dst, me)], [r], e, "%s%d" % (key, me)))

        def call():
            g.remote_dma_fused(tr, local_sem=T.sem[sem_loc])
        op("g", call, [blk(src, r) for r in others], [], sem_loc, len(others) * n)
        for r in others:
            arrive("%s%d" % (key, r), n, blk(dst, r))

    def send_all(win, key, sem_loc):
        src = (win, me * S4, me * S4 + S4)
        e = topo.engines(core, T.cores[others[0]])
        tr = transfer([src], [src] * len(others), others, e, "%s%d" % (key, me))

        def call():
            g.remote_dma_fused([tr], local_sem=T.sem[sem_loc])
        op("g", call, [src], [], sem_loc, len(e))
        for r in others:
            arrive("%s%d" % (key, r), len(e), (win, r * S4, r * S4 + S4))

    own = (me * S4, me * S4 + S4)
    op("y", lambda: g.sync.dma_start(T.snI[:], T.sn[:]), [], [full("snI")], "dsn")
    op("s", lambda: sca.dma_start(T.xb[:], T.x[:]), [], [full("xb")], "dx")
    op("y", lambda: g.sync.dma_start(T.vlI[:], T.vl[:]), [], [full("vlI")], "dvl")
    op("s", lambda: sca.dma_start(T.plI[:], T.pl[:]), [], [full("plI")], "dpl")
    vset(full("ones"), 1.0)
    ZZ = ("Z", 0, 96)
    op("v", lambda: vec.memset(T.Z[:], 0), [], [ZZ])
    for h in range(8):
        def call(r=16 * h, c=16 * (h % 2)):
            return g.sync.dma_start(T.Z[r:r + 16, :, c:c + 16], T.pl[r:r + 16, :])
        op("y", call, [], [("Z", 96 + h, 97 + h)] if h else [ZZ, ("Z", 96, 97)], "dz")
    op("g", lambda: g.iota(T.w0[:], [[1, CAP]], me * CAP, 0, allow_small_or_imprecise_dtypes=True), [], [full("w0")])
    op("g", lambda: g.affine_select(T.E2[:], T.ones[:], [[0, 2], [-1, 128]], A.is_equal, 0.0, 0, 1), [full("ones")], [full("E2")])
    for k in range(N):
        act(blk("QS", k), ("ones", 0, CAP), F.Copy, scale=0.0)
    for q in range(N):
        vts(blk("wq", q), full("w0"), float(q * S4), A.add)
    act(full("E2f"), full("E2"))
    act(full("I2"), ("E2", 0, 128), F.Copy, scale=2.0)

    vcopy(full("sn16"), full("snI"))
    def snl(q, lo=0, hi=14): return ("sn16", 14 * q + lo, 14 * q + hi)
    q0, q1, q2 = others
    vgat(blk("XS", q0), full("xb"), snl(q0))
    sgat(blk("XS", q1), full("xb"), snl(q1))
    vgat(("XS", q2 * CAP, q2 * CAP + 96), full("xb"), snl(q2, 0, 6))
    sgat(("XS", q2 * CAP + 96, q2 * CAP + CAP), full("xb"), snl(q2, 6, 14))
    vcopy(full("vl16"), full("vlI"))
    send("XS", "XW", "ax", "lx")
    op("g", lambda: g.iota(T.INV[:], [[0, S4]], 0, 0), [], [full("INV")])

    def vll(d): return ("vl16", 16 * d, 16 * d + 16)
    def sec(n, d): return (n, V * d, V * d + V)
    for d in range(3):
        sgat(sec("GH", (d + 1) % 3), full("wq"), vll((d + 1) % 3), scale=4096.0)
        sgat(sec("GL", (d + 2) % 3), full("wq"), vll((d + 2) % 3))
    vgat(blk("XW", me), full("xb"), snl(me))
    vcopy(full("pl16"), full("plI"))
    vts(full("p1"), full("plI"), 4, A.logical_shift_right)
    vts(full("p3"), full("plI"), 56.0, A.mult)
    vts(full("p2"), full("p1"), -895.0, A.mult)
    for b in range(3):
        op("v", lambda: vec.transpose(T.Z2[:, 32 * b:32 * b + 32], T.Z[:, b, :]), [("Z", 0, 104)], [("Z2", 32 * b, 32 * b + 32)])
    vtt(full("p4"), full("p3"), full("p2"), A.add)
    for d in range(3):
        vsca(full("QS"), vll(d), sec("GH", (d + 1) % 3), sec("GL", (d + 2) % 3), A.add)
        op("v", lambda: vec.tensor_tensor(T.Lw[:, d:48:3], T.Z2[:, 32 * d:32 * d + 16], T.Z2[:, 32 * d + 16:32 * d + 32], A.add),
           [("Z2", 32 * d, 32 * d + 32)], [("Lw", d, d + 1)])
        if d == 0:
            vcopy(full("plp"), full("p4"))
    send("QS", "QW", "aq", "lq")
    op("g", lambda: g.iota(T.W1[:, own[0]:own[1]], [[0, S4]], 0, 0, allow_small_or_imprecise_dtypes=True), [], [("W1",) + own])
    op("g", lambda: g.iota(T.jj[:], [[1, E]], 0, 0), [], [full("jj")])
    vcopy(full("Lp"), full("Lw"))

    def turn(win, base, ks, plan, ident="E2", mine=None):
        for p, bank, q in plan:
            o = (win, base + p * CAP, base + p * CAP + CAP)
            mm((bank, 0, CAP), rot(ks[p], ident), mine if mine and p == me else o)
            if q == "v":
                vcopy(o, (bank, 0, CAP))
            else:
                act(o, (bank, 0, CAP))

    def plan(banks, queues):
        return list(zip([p for p in [me] + others if p], banks, queues))

    if me:
        turn("XW", 0, [-p * me for p in range(N)], plan(["b0", "b1", "b2"], "sss"))
        mm(("b6", 0, CAP), rot(-me * me, "E2f"), blk("QS", me))

    P0, P1, PH = (0, 256), (256, H), (0, H)
    def sign(u, src, p, o=0): vts(at("n" + u, p, o), src, 0.0, A.is_ge, 0.5, A.subtract)
    def total(u, es):
        for e in es:
            mm(("b4", 0, M), full("I2"), ("n" + u, e * M, e * M + M), e == 0, e == 5)
    def fold(u):
        act(full("f1_" + u), ("b4", 0, M), F.Abs)
        act(full("f2_" + u), full("f1_" + u), F.Abs, bias=-4.0)
    def parity(u):
        vts(full("f3_" + u), full("f2_" + u), 2.0, A.is_equal, 0.5, A.subtract)
        for i in range(3):
            mm(("b5", i * M, i * M + M), rot(0), full("f3_" + u))
    def plc(lo, hi): return ("pl16", lo // 16, hi // 16)

    u = "1"
    sgat(("xe", H, 640), full("XW"), plc(H, 640))
    vgat(("xe", 0, H), full("XW"), plc(0, H))
    sign(u, at("xe", PH), PH)
    vgat(("xe", 640, E), full("XW"), plc(640, E))
    act(at("b1", P0), at("xe", P0, H), F.Abs, scale=4.0)
    act(at("aA1", P0), at("xe", P0), F.Abs, scale=4.0)
    sign(u, at("xe", PH, H), PH, H)
    total(u, range(6))
    act(at("b2", P1), at("xe", P1, H), F.Abs, scale=4.0)
    act(at("aA1", P1), at("xe", P1), F.Abs, scale=4.0)
    L0, L1, L01, L2 = ("L1", 0, 128), ("L1", 128, 256), ("L1", 0, 256), ("b3", H, 512)
    vtt(L01, at("aA1", P0), at("b1", P0), A.min)
    fold(u)
    act(full("aB1"), at("xe", PH, H), F.Abs, scale=4.0)
    vtt(L2, at("aA1", P1), at("b2", P1), A.min)
    vtt(("b3", 256, 384), L0, L1, A.min)
    vtt(("b3", 0, 128), L1, L2, A.min)
    vtt(("b3", 128, 256), L0, L2, A.min)
    vtt(at("mg", P1, H), at("aA1", P1), at("b3", P1), A.min)
    parity(u)
    vtt(at("mg", P0, H), at("aA1", P0), at("b3", P0), A.min)
    vtt(at("mg", PH), full("aB1"), at("b3", PH), A.min)
    for o in (0, H):
        vtt(at("z1", PH, o), at("n1", PH, o), at("b5", PH), A.mult)
    vsca(("W1",) + own, full("pl16"), full("z1"), full("mg"), A.mult)
    send_all("W1", "a1_", "l1")

    if me:
        act(blk("QW", me), ("b6", 0, CAP))
        turn("QW", 0, [-p * me for p in range(N)], plan(["b6", "b7", "b0"], "sss")[1:], "E2f")
    else:
        act(blk("QW", 0), blk("QS", 0))
    sgat(full("QG"), full("QW"), full("Lp"))
    op("y", lambda: g.sync.dma_start(T.qf[:], T.QG[0:128:16, :]), [full("QG")], [full("qf")], "dq")
    op("v", lambda: vec.tensor_copy(ind(full("INV"), full("plp")), ap(full("jj"))), [full("jj"), full("plp")], [full("INV")])
    op("y", lambda: g.sync.dma_start(T.ivI[:], T.INV[0:128:16, :]), [full("INV")], [full("ivI")], "div")

    for t, win, out, base in ((2, "W1", "W2", me * S4), (3, "W2", "R3", 0)):
        u = str(t)
        for i, q in enumerate(others):
            if t == 2 and i == 2:
                vcopy(full("qi"), full("qf"))
                vts(("ee", 0, 48), full("qi"), 12, A.logical_shift_right)
                vts(("ee", 48, 96), full("qi"), 4095, A.bitwise_and)
                vcopy(full("LL"), full("ee"))
            banks = ["b%d" % (3 * (i % 2) + j) for j in range(3)]
            turn(win, q * S4, [-p * (me - q) for p in range(N)], list(zip((1, 2, 3), banks, "vsv")))
        aA, aB, rA = "aA" + u, "aB" + u, "r" + u
        mb = {P0: at("b7", P0), P1: at("b6", P1)}
        for p in (P0, P1):
            mm(mb[p], rot(0), at("xe", p, H), True, False)
        sgat(at(rA, PH), full(win), ("LL", 24, 48))
        for p in (P0, P1):
            vgtt(at("t" + u, p), full(win), ("LL", p[0] // 16, p[1] // 16), at("xe", p), A.add)
            mm(mb[p], rot(0), at(rA, p), False, False)
        sgat(at(rA, P0, H), full(win), ("LL", 72, 88))
        mm(mb[P0], rot(0), at(rA, P0, H), False, True)
        vgtt(at("m" + u, P0), full(win), ("LL", 48, 64), at("t" + u, P0), A.add)
        vgat(at(rA, P1, H), full(win), ("LL", 88, 96))
        mm(mb[P1], rot(0), at(rA, P1, H), False, True)
        vgtt(at("m" + u, P1), full(win), ("LL", 64, 72), at("t" + u, P1), A.add)
        act(at(aA, P0), at("m" + u, P0), F.Abs, scale=4.0)
        if t == 2:
            vcopy(full("iv"), full("ivI"))
        for p in (P0, P1):
            sign(u, at("m" + u, p), p)
        total(u, range(3))
        act(at("b1", P0), mb[P0], F.Abs, scale=4.0)
        act(at(aA, P1), at("m" + u, P1), F.Abs, scale=4.0)
        act(at("b2", P1), mb[P1], F.Abs, scale=4.0)
        vts(at(aA, P0), at(aA, P0), 4.0 * B, A.min)
        L0, L1, L01, L2 = ("L" + u, 0, 128), ("L" + u, 128, 256), ("L" + u, 0, 256), ("b3", H, 512)
        vtt(L01, at(aA, P0), at("b1", P0), A.min)
        sign(u, mb[P0], P0, H)
        vtt(L2, at(aA, P1), at("b2", P1), A.min)
        sign(u, mb[P1], P1, H)
        total(u, range(3, 6))
        for p in (P0, P1):
            act(at(aB, p), mb[p], F.Abs, scale=4.0)
        vtt(("b3", 256, 384), L0, L1, A.min)
        vtt(("b3", 0, 128), L1, L2, A.min)
        vtt(("b3", 128, 256), L0, L2, A.min)
        fold(u)
        vtt(at("b2", P1), at(aA, P1), at("b3", P1), A.min)
        vtt(at("b2", P0), at(aA, P0), at("b3", P0), A.min)
        vtt(at("b0", PH), full(aB), at("b3", PH), A.min)
        parity(u)
        vtt(at("z" + u, PH, H), at("n" + u, PH, H), at("b2", PH), A.mult)
        vtt(at("z" + u, PH), at("n" + u, PH), at("b0", PH), A.mult)
        for o in (H, 0):
            vtt(at("Rd", PH, o), at("z" + u, PH, o), at("b5", PH), A.mult)
        k = 30
        sgat((out, base + 16 * k, base + S4), full("Rd"), ("iv", k, 56))
        vgat((out, base, base + 16 * k), full("Rd"), ("iv", 0, k))
        if t == 2:
            send_all("W2", "a2_", "l2")
        else:
            send("R3", "VW", "a3_", "l3")

    if me:
        turn("VW", 0, [q * me for q in range(N)], plan(["b0", "b1", "b2"], "svs"), mine=blk("R3", me))
    else:
        vcopy(blk("VW", 0), blk("R3", 0))
    P, Q = (0, 128), (128, 256)
    sgat(at("yt", P, 2 * V), full("VW"), ("vl16", 32, 40))
    vgtt(at("yt", P), full("VW"), ("vl16", 0, 8), at("xb", P), A.add)
    vgtt(at("yt", Q), full("VW"), ("vl16", 8, 16), at("xb", Q), A.add)
    sgat(at("yt", Q, V), full("VW"), ("vl16", 24, 32))
    vgtt(at("yt", P, V), full("VW"), ("vl16", 16, 24), at("yt", P), A.add)
    mm(("b3", 0, 128), rot(0), at("yt", Q, V), True, False)
    sgat(at("yt", Q, 2 * V), full("VW"), ("vl16", 40, 48))
    mm(("b3", 0, 128), rot(0), at("yt", Q, 2 * V), False, True)
    vtt(at("yo", P), at("yt", P, V), at("yt", P, 2 * V), A.add)
    vtt(at("yo", Q), at("yt", Q), ("b3", 0, 128), A.add)
    op("y", lambda: g.sync.dma_start(T.y[:, 0:128], T.yo[:, 0:128]), [("yo", 0, 128)], [], "dy0")
    op("s", lambda: sca.dma_start(T.y[:, 128:256], T.yo[:, 128:256]), [("yo", 128, 256)], [], "dy1")
    finish()
